import numpy as np, ml_dtypes
CORES = [16,18,20,22]
N = 4
BF = ml_dtypes.bfloat16
def f(rng, *shape):
    return (rng.standard_normal(shape, dtype=np.float32) * np.exp2(rng.integers(-2, 3, shape[:-1] + (1,)))).astype(BF)
def wide(rng, *shape):
    v = f(rng, *shape).astype(np.float32); k = shape[:-2] + (1, shape[-1])
    return (v * np.exp2(rng.integers(-6, 7, k)) * (rng.random(k) > 0.0625)).astype(BF)
M, K, TR, CAP = 4096, 64, 4, 384
D = 16 * K
def hashes(s, n):
    lo = ((s & 4095) + 1597 * n) & 4095; b = ((s >> 12) + ((lo * lo) >> 6)) & 4095
    return (lo + ((b * b) >> 6)) & 4095, b
def seed_of(a, b, n):
    lo = (a - ((b * b) >> 6)) & 4095
    return ((b - ((lo * lo) >> 6)) & 4095) * 4096 + ((lo - 1597 * n) & 4095)
def owners(t, s):
    a, b = hashes(np.asarray(s, np.int64)[..., None], (TR + 1) * np.arange(K)); w = (a * N) >> 12
    return np.where(b < t[w], w, t[N + w]).astype(np.int64)
def loads(t, s):
    o = owners(t, s); return np.stack([np.sum(o == q, -1) for q in range(N)], -1)
def sixteen(rng, t, keep=()):
    m = 16 - len(keep); kept = np.array(keep, np.int64); base = np.sum(loads(t, kept), 0)
    pool = rng.integers(0, 1 << 24, 1024); c = loads(t, pool); ok = np.flatnonzero(np.all(c * m <= CAP - base, 1)); j = np.arange(m)
    for u in range(m):
        if np.all(np.sum(c[j], 0) + base <= CAP): break
        j[u] = rng.choice(ok)
    return rng.permutation(np.concatenate([pool[j], kept]))
def ranks(rng, least):
    return np.concatenate([rng.integers(least, 4097, N), rng.permutation(N)]).astype(np.int64)
def absent(rng):
    w = rng.permutation(N); t = np.zeros(2 * N, np.int64)
    t[w] = (8192 * np.arange(N) + N - 1) // (2 * (N - 1)); t[N + w] = np.roll(w, -1); return t
def history(rng, dens):
    w = np.zeros((N, 128, M), np.float32)
    for q in range(N):
        for r in range(N):
            w[q] += np.float32(2 ** r) * (rng.random((128, M), dtype=np.float32) < dens[r][:, None])
    return w.astype(BF)
def seeds(rng, rk):
    return np.stack([np.stack([sixteen(rng, rk[g]) for g in range(8)]) for r in range(N)])
def complete(rng, rk, sd, dens=None):
    if dens is None: dens = rng.choice(np.array([0.1, 0.5, 0.9]), (N, 128))
    return {"sd": np.reshape(sd, (N, 128, 1)).astype(np.int32), "rk": np.stack([rk] * N).astype(np.int32), "thr": rng.integers(0, 4097, (N, 8, M)).astype(np.int32),
            "ali": rng.integers(0, M, (N, 8, M)).astype(np.int32), "seen": history(rng, dens), "vec": f(rng, N, 128, M)}
def setup_inputs(rng):
    rk = np.stack([ranks(rng, 2800) for g in range(8)]); return complete(rng, rk, seeds(rng, rk))
def setup_inputs_full(rng):
    o0 = rng.integers(0, N); rk = []
    for g in range(8):
        o = (o0 + g) % N; t = np.concatenate([rng.integers(3577 - 40, 3577 + 41, N), np.full(N, o)]).astype(np.int64); t[o] = 4096; rk.append(t)
    rk = np.stack(rk); sd = seeds(rng, rk); C = CAP // 16
    far = rng.integers(0, N, 8); h = rng.permutation(8); far[h[0]] = 0; far[h[1]] = rng.integers(1, N)
    for g in range(8):
        o = (o0 + g) % N; r = (o + far[g]) % N
        pool = rng.integers(0, 1 << 24, 4096); c = loads(rk[g], pool); fine = np.all(np.delete(c, o, 1) <= C, 1); s = []
        for i in range(8):
            x = rng.integers(-2, 3)
            for v in (C + x, C - x): s.append(pool[rng.choice(np.flatnonzero(fine & (c[:, o] == v)))])
        sd[r, g] = rng.permutation(np.array(s))
    return complete(rng, rk, sd)
def setup_inputs_edges(rng):
    rk, tie = [], []
    for g in range(8):
        t = ranks(rng, 3500); w = rng.permutation(N)[:4]; t[w[0]] = 0; t[N + w[0]] = w[1]; t[w[1]] = 0; t[N + w[1]] = w[0]; t[w[2]] = rng.integers(3500, 4096); t[N + w[2]] = w[0]; t[w[3]] = 4096; rk.append(t)
        tie.append(seed_of(int(w[2]) * (4096 // N) + int(rng.integers(0, 4096 // N)), int(t[w[2]]), (TR + 1) * int(rng.integers(0, K))))
    rk = np.stack(rk); sd = np.stack([np.stack([sixteen(rng, rk[g], (0, (1 << 24) - 1, tie[g])) for g in range(8)]) for r in range(N)])
    d = complete(rng, rk, sd); z = rng.integers(0, 4, (N, 8, M)); thr = np.where(z == 0, 0, np.where(z == 1, 4096, d["thr"])); z = rng.integers(0, 4, (N, 8, M))
    ali = np.where(z == 0, 0, np.where(z == 1, M - 1, np.where(z == 2, np.arange(M), d["ali"])))
    for r in range(N):
        for g in range(8):
            q = owners(rk[g], sd[r, g])[:, ::4]; a, b = hashes(sd[r, g][:, None], ((TR + 1) * np.arange(K) + 1)[None, ::4]); e = (a * M) >> 12
            thr[q, g, e] = b; ali[q, g, e] = M - 1 - e
    d["thr"] = thr.astype(np.int32); d["ali"] = ali.astype(np.int32); return d
def setup_inputs_hot(rng):
    rk = np.stack([ranks(rng, 2800) for g in range(8)]); sd = seeds(rng, rk)
    for g in range(8):
        pool = rng.integers(0, 1 << 24, 1024); sd[rng.integers(0, N), g] = pool[rng.choice(np.flatnonzero(np.all(loads(rk[g], pool) <= CAP // 16, 1)))]
    d = complete(rng, rk, sd); h = rng.integers(0, M, (N, 8, 1)); h[:, 0] = 0; h[:, 7] = M - 1
    d["thr"] = rng.integers(0, 512, (N, 8, M)).astype(np.int32); d["ali"] = (h + np.zeros((1, 1, M), np.int64)).astype(np.int32); return d
def setup_inputs_avid(rng):
    rk = np.stack([absent(rng) for g in range(8)]); dens = rng.choice(np.array([0, 0.97, 1.0]), (N, 128)); dens[rng.integers(0, N)] = 1
    return complete(rng, rk, seeds(rng, rk), dens)
def setup_inputs_spread(rng):
    d = setup_inputs(rng); d["vec"] = wide(rng, N, 128, M); d["thr"] = (4096 >> rng.integers(0, 14, (N, 8, M))).astype(np.int32); return d
def check_inputs(d):
    bad = []
    try:
        sd, rk = d["sd"].astype(np.int64), d["rk"].astype(np.int64); w = d["seen"].astype(np.float32)
        if not ((sd >= 0) & (sd < 1 << 24)).all(): bad.append("seed")
        if not (rk == rk[:1]).all(): bad.append("rk alike on all ranks")
        if not ((rk[..., :N] >= 0) & (rk[..., :N] <= 4096) & (rk[..., N:] >= 0) & (rk[..., N:] < N)).all(): bad.append("rk")
        if not ((d["thr"] >= 0) & (d["thr"] <= 4096)).all(): bad.append("thr")
        if not ((d["ali"] >= 0) & (d["ali"] < M)).all(): bad.append("ali")
        if not ((w >= 0) & (w < 2 ** N) & (w == np.floor(w))).all(): bad.append("seen")
        if not np.isfinite(d["vec"].astype(np.float32)).all(): bad.append("finite")
        if not bad and any((np.sum(loads(rk[r, g], sd[r, 16 * g:16 * g + 16, 0]), 0) > CAP).any() for r in range(N) for g in range(8)): bad.append("cap")
    except Exception:
        bad.append("unreadable")
    return bad
def reference(sd, rk, thr, ali, seen, vec):
    chosen = np.zeros((N, 128, K), np.float32); y = np.zeros((N, 128, D), vec.dtype); n = (TR + 1) * np.arange(K); row = np.arange(16)[:, None]
    for r in range(N):
        for g in range(8):
            s = sd[r, 16 * g:16 * g + 16].astype(np.int64)
            q = owners(rk[r, g].astype(np.int64), s[:, 0])
            x = np.zeros((16, K), np.int64); done = np.zeros((16, K), bool)
            for i in range(1, TR + 1):
                a, b = hashes(s, n + i); e = (a * M) >> 12
                c = np.where(b < thr[q, g, e], e, ali[q, g, e]).astype(np.int64)
                known = (seen[q, 16 * g + row, c].astype(np.float32).astype(np.int64) >> r) & 1
                x = np.where(done, x, c); done = done | (known == 0)
            chosen[r, 16 * g:16 * g + 16] = q * M + x
            y[r, 16 * g:16 * g + 16] = vec[q.T.reshape(-1), 16 * g + row, x.T.reshape(-1)]
    return {"chosen": chosen, "y": y}

@@ -1,0 +1,398 @@
+from concourse.bass import DstId, RemoteDMATransfer
+from concourse.mybir import AluOpType as OP, ActivationFunctionType as AF
+
+M, K = 4096, 64
+H = M // 2
+FROW = [0, 2, 1, 3]
+V_FILL = 5120
+P_FILL = 7168
+
+SCRATCH = {
+    "fw": ("sbuf", [128, 4 * M], "bfloat16"),
+    "sw": ("sbuf", [128, 4 * M], "bfloat16"),
+    "vw": ("sbuf", [128, 4 * M], "bfloat16"),
+    "fl": ("dram", [4, 128, 1024], "bfloat16"),
+    "ta": ("sbuf", [128, 512], "int32"),
+    "ft": ("sbuf", [128, 1024], "bfloat16"),
+    "sdi": ("sbuf", [128, 1], "int32"),
+    "shi": ("sbuf", [128, 1], "int32"),
+    "sdf": ("sbuf", [128, 1], "float32"),
+    "cf": ("sbuf", [128, 1], "float32"),
+    "rki": ("sbuf", [8, 8], "int32"),
+    "rkf": ("sbuf", [8, 8], "float32"),
+    "f8": ("sbuf", [8, 128], "float32"),
+    "gs": ("sbuf", [8, 128], "float32"),
+    "rkc": ("sbuf", [128, 8], "float32"),
+    "a4": ("sbuf", [128, 4], "float32"),
+    "dj": ("sbuf", [128, 4], "float32"),
+    "j4": ("sbuf", [128, 4], "float32"),
+    "ob": ("sbuf", [128, 128], "bfloat16"),
+    "cm": ("sbuf", [128, 2336], "bfloat16"),
+    "idt": ("sbuf", [128, 128], "bfloat16"),
+    "n1": ("sbuf", [128, 320], "int32"),
+    "hx": ("sbuf", [128, 320], "int32"),
+    "hl": ("sbuf", [128, 320], "int32"),
+    "hs": ("sbuf", [128, 320], "float32"),
+    "hm": ("sbuf", [128, 320], "int32"),
+    "hs2": ("sbuf", [128, 320], "int32"),
+    "hb": ("sbuf", [128, 320], "int32"),
+    "ht": ("sbuf", [128, 320], "float32"),
+    "ht2": ("sbuf", [128, 320], "int32"),
+    "ha": ("sbuf", [128, 320], "int32"),
+    "of": ("sbuf", [128, 256], "float32"),
+    "oh": ("sbuf", [128, 256], "float32"),
+    "og": ("sbuf", [128, 192], "float32"),
+    "oge": ("sbuf", [128, 192], "float32"),
+    "op": ("sbuf", [128, 256], "float32"),
+    "o2": ("sbuf", [128, 128], "float32"),
+    "q4": ("sbuf", [128, 64], "float32"),
+    "q4b": ("sbuf", [128, 64], "bfloat16"),
+    "off": ("sbuf", [128, 256], "float32"),
+    "l1": ("sbuf", [128, 256], "uint16"),
+    "l2": ("sbuf", [128, 256], "uint16"),
+    "l3": ("sbuf", [128, 64], "uint16"),
+    "acc": ("sbuf", [128, 256], "float32"),
+    "dd": ("sbuf", [128, 256], "float32"),
+    "mm": ("sbuf", [128, 256], "float32"),
+    "cc": ("sbuf", [128, 256], "float32"),
+    "dc": ("sbuf", [128, 192], "float32"),
+    "vi": ("sbuf", [128, 64], "int32"),
+    "vb": ("sbuf", [128, 64], "int32"),
+    "mk": ("sbuf", [128, 192], "float32"),
+    "pp": ("sbuf", [128, 256], "float32"),
+    "p2": ("sbuf", [128, 128], "float32"),
+    "xx": ("sbuf", [128, 64], "float32"),
+    "yt": ("sbuf", [128, 1024], "bfloat16"),
+    "psr": ("psum", [128, 512], "float32"),
+    "psk": ("psum", [128, 512], "float32"),
+}
+for _i in range(4):
+    SCRATCH["ga%d" % _i] = ("sbuf", [128, 1024], "bfloat16")
+    SCRATCH["gb%d" % _i] = ("sbuf", [128, 1024], "bfloat16")
+    SCRATCH["ps%d" % _i] = ("psum", [128, 512], "float32")
+
+SEMAPHORES = ["v", "a", "p", "t", "ldt", "lds", "ldr", "sn0", "sn1", "vc0", "vc1", "fx", "st", "lr",
+              "aft0", "aft1", "aft2", "aft3", "asn", "avc", "hs1", "hv0", "hv1"]
+
+
+def helper_of(core, T, topo):
+    free = [c for c in topo.cores_of(core) if T.rank_of(c) is None and topo.die(c) == topo.die(core)]
+    mine = [c for c in T.cores if topo.chip(c) == topo.chip(core) and topo.die(c) == topo.die(core)]
+    return free[mine.index(core)]
+
+
+def spread(g, T, topo, core, dsts, src, name, dst_ap):
+    ids = []
+    for d in dsts:
+        rid, pid, _s = topo.addr(d)
+        ids.append(DstId(rid=rid, pnc=pid))
+    mask = topo.mask(core, dsts[0])
+    for d in dsts:
+        mask &= topo.mask(core, d)
+    g.remote_dma_fused([RemoteDMATransfer(dst_ids=ids, dma_engine_mask=mask, remote_sem=T.sem[name],
+                                          srcs=[src], dsts=[dst_ap for d in dsts], alu_op=0)], local_sem=T.sem.lr)
+    return len(topo.engines(core, dsts[0]))
+
+
+def helper_program(g, core, T, topo, owner):
+    r = T.rank_of(owner)
+    ne = len(topo.engines(owner, core))
+    dsts = [c for c in T.cores if c != owner]
+    b = M * r
+    n = 0
+    g.wait_ge(T.sem.hs1, ne)
+    n += spread(g, T, topo, core, dsts, T.sw[:, b + H:b + M], "asn", T.sw[:, b + H:b + M])
+    g.wait_ge(T.sem.hv0, ne)
+    n += spread(g, T, topo, core, dsts, T.vw[:, b:b + H], "avc", T.vw[:, b:b + H])
+    g.wait_ge(T.sem.hv1, ne)
+    n += spread(g, T, topo, core, dsts, T.vw[:, b + H:b + M], "avc", T.vw[:, b + H:b + M])
+    g.wait_ge(T.sem.lr, n)
+
+
+def rank_program(g, core, T, topo):
+    rank = T.rank_of(core)
+    if rank is None:
+        for c in T.cores:
+            if c in topo.cores_of(core) and helper_of(c, T, topo) == core:
+                helper_program(g, core, T, topo, c)
+        return
+
+    others = [c for c in T.cores if c != core]
+    hc = helper_of(core, T, topo)
+    b0 = M * rank
+    engs = {"v": g.vector, "a": g.scalar, "p": g, "t": g.tensor, "s": g.sync}
+    cnt = {}
+    seen = {k: {} for k in engs}
+
+    def need(q, toks):
+        for name, val in toks:
+            if seen[q].get(name, 0) < val:
+                engs[q].wait_ge(T.sem[name], val)
+                seen[q][name] = val
+
+    def done(q, ins, n=1, sem=None):
+        s = sem or q
+        ins.then_inc(T.sem[s], n)
+        cnt[s] = cnt.get(s, 0) + n
+        return (s, cnt[s])
+
+    v, a, t = g.vector, g.scalar, g.tensor
+
+    def TT(out, x, y, op, *deps):
+        need("v", deps)
+        return done("v", v.tensor_tensor(out, x, y, op))
+
+    def TS(out, x, s1, op0, s2, op1, *deps):
+        need("v", deps)
+        if op1 is None:
+            return done("v", v.tensor_scalar(out, x, s1, None, op0))
+        return done("v", v.tensor_scalar(out, x, s1, s2, op0, op1))
+
+    def CP(out, x, *deps):
+        need("v", deps)
+        return done("v", v.tensor_copy(out, x))
+
+    def FILL(ap, c):
+        return done("v", v.memset(ap, c))
+
+    def dma(q, out, x, sem, *deps):
+        need(q, deps)
+        return done(q, engs[q].dma_start(out, x), 16, sem)
+
+    dma("s", T.ta[:, 0:256], T.thr[:, :], "ldt")
+    dma("s", T.sdi[:, :], T.sd[:, :], "lds")
+    ld_t = dma("a", T.ta[:, 256:512], T.ali[:, :], "ldt")
+    ld_r = dma("a", T.rki[:, :], T.rk[:, :], "ldr")
+    ld_s = ("lds", 16)
+    ld_s1 = dma("s", T.sw[:, b0 + H:b0 + M], T.seen[:, H:M], "sn1")
+    ld_s0 = dma("s", T.sw[:, b0:b0 + H], T.seen[:, 0:H], "sn0")
+    ld_v0 = dma("s", T.vw[:, b0:b0 + H], T.vec[:, 0:H], "vc0")
+    ld_v1 = dma("s", T.vw[:, b0 + H:b0 + M], T.vec[:, H:M], "vc1")
+
+    t_f8 = FILL(T.f8[:, :], 1.0)
+    t_ob = FILL(T.ob[:, :], 1.0)
+    t_f0 = FILL(T.fw[:, 0:2048], 1.0)
+    t_cm = FILL(T.cm[:, :], 0.0)
+
+    def SEL(out, x, pattern, op, base, ch, *deps):
+        need("p", deps)
+        return done("p", g.affine_select(out, x, pattern, op, 0.0, base, ch))
+
+    t_gs = SEL(T.gs[:, :], T.f8[:, :], [[1, 128]], OP.is_ge, 0, -16, t_f8)
+    t_gs = SEL(T.gs[:, :], T.gs[:, :], [[-1, 128]], OP.is_ge, 15, 16, t_gs)
+    t_n1 = done("p", g.iota(T.n1[:, :], [[1597, 5], [5 * 1597, 64]], -(1 << 23), 0))
+    t_j4 = done("p", g.iota(T.j4[:, :], [[M, 4]], 0, 0, allow_small_or_imprecise_dtypes=True))
+    mid = (V_FILL + P_FILL) // 2
+    t_pf0 = done("p", g.iota(T.fw[:, V_FILL:mid], [[0, mid - V_FILL]], 1, 0, allow_small_or_imprecise_dtypes=True))
+
+    fills = {}
+    need("a", [t_f0])
+    c0 = P_FILL
+    af = []
+    while c0 < 4 * M:
+        c1 = min(4 * M, (c0 // 2048 + 1) * 2048)
+        af.append((c0, c1, done("a", a.activation(T.fw[:, c0:c1], T.fw[:, 0:c1 - c0], AF.Copy))))
+        c0 = c1
+
+    t_hi = CP(T.ft[:, 0:512], T.ta[:, :], ld_t)
+    t_ft = TT(T.ft[:, 512:1024], T.ta[:, :], T.ft[:, 0:512], OP.subtract, t_hi)
+
+    t_sdf = CP(T.sdf[:, :], T.sdi[:, :], ld_s)
+    t_shi = TS(T.shi[:, :], T.sdi[:, :], 12, OP.logical_shift_right, None, None)
+    t_rkf = CP(T.rkf[:, :], T.rki[:, :], ld_r)
+    t_cf = TS(T.cf[:, :], T.shi[:, :], 64.0, OP.mult, -float(1 << 22), OP.add, t_shi)
+    need("t", [t_rkf, t_gs])
+    t_psr = done("t", t.matmul(T.psr[:, 0:8], T.gs[:, :], T.rkf[:, :], True, True))
+    t_f1 = FILL(T.fw[:, 2048:V_FILL], 1.0)
+
+    need("p", [t_ft])
+    lr = spread(g, T, topo, core, others, T.ft[:, :], "aft%d" % rank, T.fl[rank])
+    need("p", [ld_s1])
+    lr += spread(g, T, topo, core, [hc], T.sw[:, b0 + H:b0 + M], "hs1", T.sw[:, b0 + H:b0 + M])
+    need("p", [ld_s0])
+    lr += spread(g, T, topo, core, others, T.sw[:, b0:b0 + H], "asn", T.sw[:, b0:b0 + H])
+    t_pf1 = done("p", g.iota(T.fw[:, mid:P_FILL], [[0, P_FILL - mid]], 1, 0, allow_small_or_imprecise_dtypes=True))
+    wt, wa = 2048, 2192
+
+    def diag(w, u):
+        return T.cm[:, w + 15 - u:w + 143 - u]
+
+    SEL(T.cm[:, wt + 15:wt + 143:16], T.ob[:, 0:8], [[-16, 8]], OP.is_ge, 0, 1, t_ob, t_cm)
+    t_w = SEL(T.cm[:, wa + 15:wa + 143:16], T.ob[:, 0:8], [[-16, 8]], OP.is_ge, -2, 1)
+    SEL(T.cm[:, wt + 15:wt + 143:16], T.cm[:, wt + 15:wt + 143:16], [[16, 8]], OP.is_ge, 1, -1, t_w)
+    SEL(T.cm[:, wa + 15:wa + 143:16], T.cm[:, wa + 15:wa + 143:16], [[16, 8]], OP.is_ge, 3, -1)
+    SEL(T.idt[:, :], T.ob[:, :], [[-1, 128]], OP.is_equal, 0, 1)
+    t_con = SEL(T.cm[:, 0:2048:16], T.ob[:, :], [[-1, 16], [-16, 8]], OP.is_equal, 0, 1)
+    ne = len(topo.engines(core, hc))
+    need("p", [ld_v0])
+    lr += spread(g, T, topo, core, [hc], T.vw[:, b0:b0 + H], "hv0", T.vw[:, b0:b0 + H])
+    need("p", [ld_v1])
+    lr += spread(g, T, topo, core, [hc], T.vw[:, b0 + H:b0 + M], "hv1", T.vw[:, b0 + H:b0 + M])
+
+    regions = [(0, 2048, t_f0), (2048, V_FILL, t_f1), (V_FILL, mid, t_pf0), (mid, P_FILL, t_pf1)] + af
+    t_fx = None
+    for q in range(4):
+        lo, hi = M * q, M * q + M
+        deps = [tok for (x0, x1, tok) in regions if x0 < hi and lo < x1]
+        if q == 0:
+            deps += [af[-1][2]]
+        deps += [t_ft] if q == rank else [("aft%d" % q, len(topo.engines(T.cores[q], core)))]
+        for f in range(4):
+            x = T.ft[:, 256 * f:256 * f + 256] if q == rank else T.fl[q][:, 256 * f:256 * f + 256]
+            t_fx = dma("s", T.fw[FROW[f]::16, lo:hi], x, "fx", *deps)
+
+    tok = {}
+
+    def step(s, c0, c1):
+        c = slice(c0, c1)
+        k = lambda n: tok[(n, c0)]
+        if s == 0:
+            r = TS(T.hx[:, c], T.n1[:, c], T.sdf[:, 0:1], OP.add, None, None, t_n1, t_sdf)
+        elif s == 1:
+            r = TS(T.hl[:, c], T.hx[:, c], 4095, OP.bitwise_and, None, None, k(0))
+        elif s == 2:
+            r = TT(T.hs[:, c], T.hl[:, c], T.hl[:, c], OP.mult, k(1))
+        elif s == 3:
+            r = TS(T.hm[:, c], T.hl[:, c], 64.0, OP.mult, -float(1 << 22), OP.add, k(1))
+        elif s == 4:
+            r = TS(T.hs2[:, c], T.hs[:, c], T.cf[:, 0:1], OP.add, None, None, k(2), t_cf)
+        elif s == 5:
+            r = TS(T.hb[:, c], T.hs2[:, c], 6, OP.arith_shift_right, 4095, OP.bitwise_and, k(4))
+        elif s == 6:
+            r = TT(T.ht[:, c], T.hb[:, c], T.hb[:, c], OP.mult, k(5))
+        elif s == 7:
+            r = TT(T.ht2[:, c], T.ht[:, c], T.hm[:, c], OP.add, k(6), k(3))
+        else:
+            r = TS(T.ha[:, c], T.ht2[:, c], 6, OP.arith_shift_right, 4095, OP.bitwise_and, k(7))
+        tok[(s, c0)] = r
+        return r
+
+    def O(s):
+        return step(s, 0, 64)
+
+    def Ca(s):
+        return step(s, 64, 192)
+
+    def Cb(s):
+        return step(s, 192, 320)
+
+    O(0); Ca(0); O(1); Ca(1); O(2); Ca(2); O(3); O(4)
+    t_a4 = TS(T.a4[:, :], T.psr[:, 4:8], float(M), OP.mult, None, None, t_psr)
+    t_rkc = CP(T.rkc[:, :], T.psr[:, 0:8])
+    O(5)
+    t_dj = TT(T.dj[:, :], T.j4[:, :], T.a4[:, :], OP.subtract, t_j4, t_a4)
+    Ca(3)
+    O(6)
+    for j in range(4):
+        tf = TS(T.of[:, 64 * j:64 * j + 64], T.hb[:, 0:64], T.rkc[:, j:j + 1], OP.is_lt, T.dj[:, j:j + 1], OP.mult, t_rkc, t_dj, tok[(5, 0)])
+    O(7)
+    for j in range(4):
+        th = TS(T.oh[:, 64 * j:64 * j + 64], T.of[:, 64 * j:64 * j + 64], T.a4[:, j:j + 1], OP.add, None, None, tf)
+    O(8)
+    TS(T.op[:, 192:256], T.of[:, 0:64], T.a4[:, 0:1], OP.add, None, None)
+    tg = TT(T.og[:, :], T.oh[:, 64:256], T.oh[:, 0:192], OP.subtract, th)
+    for j in range(1, 4):
+        te = TS(T.oge[:, 64 * j - 64:64 * j], T.ha[:, 0:64], float(1024 * j), OP.is_ge, None, None, tok[(8, 0)])
+    Ca(4)
+    tp = TT(T.op[:, 0:192], T.oge[:, :], T.og[:, :], OP.mult, te, tg)
+    Ca(5)
+    tp = TT(T.o2[:, :], T.op[:, 0:128], T.op[:, 128:256], OP.add, tp)
+    Ca(6)
+    t_q4 = TT(T.q4[:, :], T.o2[:, 0:64], T.o2[:, 64:128], OP.add, tp)
+    Ca(7)
+    t_q4b = CP(T.q4b[:, :], T.q4[:, :], t_q4)
+    Ca(8)
+
+    def offs(i):
+        return TT(T.off[:, 64 * i:64 * i + 64], T.ha[:, 64 * i + 64:64 * i + 128], T.q4[:, :], OP.add, t_q4,
+                  tok[(8, 64 if i < 2 else 192)])
+
+    Cb(0)
+    offs(0); x = offs(1)
+    Cb(1)
+    t_l1a = CP(T.l1[:, 0:128], T.off[:, 0:128], x)
+    Cb(2); Cb(3); Cb(4); Cb(5); Cb(6); Cb(7); Cb(8)
+    offs(2); x = offs(3)
+    t_l1b = CP(T.l1[:, 128:256], T.off[:, 128:256], x)
+
+    def gather_a(out, win, lst, scale, *deps):
+        need("a", deps)
+        return done("a", a.activation(out, win.indirect(lst), AF.Copy, scale=scale))
+
+    def gather_v(out, win, lst, scale, *deps):
+        need("v", deps)
+        if scale == 1.0:
+            return done("v", v.tensor_copy(out, win.indirect(lst)))
+        return done("v", v.tensor_scalar(out, win.indirect(lst), scale, None, OP.mult))
+
+    G = [None] * 4
+    G[0] = gather_a(T.ga0[:, :], T.fw[:, :], T.l1[:, 0:64], 1.0, t_fx, t_l1a)
+    G[1] = gather_a(T.ga1[:, :], T.fw[:, :], T.l1[:, 64:128], 1.0)
+    G[3] = gather_a(T.ga3[:, :], T.fw[:, :], T.l1[:, 192:256], 1.0, t_l1b)
+    G[2] = gather_v(T.ga2[:, :], T.fw[:, :], T.l1[:, 128:192], 1.0, t_fx, t_l1b)
+    PT = [None] * 4
+    for i in range(4):
+        need("t", [G[i], t_con, t_q4b])
+        src, ps = T["ga%d" % i], T["ps%d" % i]
+        for u in range(16):
+            t.matmul(ps[:, 0:64], diag(wt, u), src[:, u::16], u == 0, u == 15)
+        for u in range(16):
+            t.matmul(ps[:, 64:128], diag(wa, u), src[:, u::16], u == 0, False)
+        PT[i] = done("t", t.matmul(ps[:, 64:128], T.idt[:, :], T.q4b[:, :], False, True))
+
+    def decide(pair):
+        tk = {}
+        for i in pair:
+            c, ps = slice(64 * i, 64 * i + 64), T["ps%d" % i]
+            TT(T.acc[:, c], ps[:, 0:64], T.hb[:, 64 * i + 64:64 * i + 128], OP.is_gt, PT[i])
+            tk[i] = TT(T.dd[:, c], T.off[:, c], ps[:, 64:128], OP.subtract)
+        for i in pair:
+            c = slice(64 * i, 64 * i + 64)
+            tk[i] = TT(T.mm[:, c], T.acc[:, c], T.dd[:, c], OP.mult, tk[i])
+        for i in pair:
+            c, ps = slice(64 * i, 64 * i + 64), T["ps%d" % i]
+            tk[i] = TT(T.cc[:, c], T.mm[:, c], ps[:, 64:128], OP.add, tk[i])
+        for i in pair:
+            c = slice(64 * i, 64 * i + 64)
+            tk[i] = CP(T.l2[:, c], T.cc[:, c], tk[i])
+        return tk
+
+    d01 = decide([0, 1])
+    d23 = decide([2, 3])
+
+    all_s = ("asn", 3 * 2 * ne)
+    E = [[], [], [], []]
+    E[0].append(gather_a(T.gb0[:, :], T.sw[:, :], T.l2[:, 0:64], 4096.0, all_s, ld_s0, ld_s1, d01[0]))
+    E[1].append(gather_a(T.gb1[:, :], T.sw[:, :], T.l2[:, 64:128], 256.0, d01[1]))
+    E[2].append(gather_v(T.gb2[:, :], T.sw[:, :], T.l2[:, 128:192], 16.0, all_s, ld_s0, ld_s1, d23[2]))
+    E[3].append(gather_a(T.gb3[:, 0:512], T.sw[:, :], T.l2[:, 192:224], 1.0, d23[3]))
+    E[3].append(gather_v(T.gb3[:, 512:1024], T.sw[:, :], T.l2[:, 224:256], 1.0, d23[3]))
+    t_dc = TT(T.dc[:, :], T.cc[:, 64:256], T.cc[:, 0:192], OP.subtract)
+    CP(T.pp[:, 192:256], T.cc[:, 0:64])
+    t_psk = None
+    for i in range(4):
+        need("t", E[i])
+        src = T["gb%d" % i]
+        for u in range(16):
+            ins = t.matmul(T.psk[:, 0:64], T.cm[:, 127 * u:127 * u + 128], src[:, u::16], i + u == 0, i == 3 and u == 15)
+    t_psk = done("t", ins)
+
+    x = CP(T.vi[:, :], T.psk[:, 0:64], t_psk)
+    x = TS(T.vb[:, :], T.vi[:, :], rank, OP.logical_shift_right, 0x1111, OP.bitwise_and, x)
+    y = None
+    for j, lim in enumerate((0x1000, 0x1100, 0x1110)):
+        y = TS(T.mk[:, 64 * j:64 * j + 64], T.vb[:, :], float(lim), OP.is_ge, None, None, x)
+    x = TT(T.pp[:, 0:192], T.mk[:, :], T.dc[:, :], OP.mult, y, t_dc)
+    x = TT(T.p2[:, :], T.pp[:, 0:128], T.pp[:, 128:256], OP.add, x)
+    t_x = TT(T.xx[:, :], T.p2[:, 0:64], T.p2[:, 64:128], OP.add, x)
+    t_l3 = CP(T.l3[:, :], T.xx[:, :], t_x)
+    dma("s", T.chosen[:, :], T.xx[:, :], "st", t_x)
+
+    all_v = ("avc", 3 * 2 * ne)
+    ya = gather_a(T.yt[:, 512:1024], T.vw[:, :], T.l3[:, 32:64], 1.0, all_v, ld_v0, ld_v1, t_l3)
+    yv = gather_v(T.yt[:, 0:512], T.vw[:, :], T.l3[:, 0:32], 1.0, all_v, ld_v0, ld_v1, t_l3)
+    dma("s", T.y[:, 0:512], T.yt[:, 0:512], "st", yv)
+    t_st = dma("a", T.y[:, 512:1024], T.yt[:, 512:1024], "st", ya)
+
+    need("p", [("lr", lr)])
+    need("s", [t_st] + [(s, cnt[s]) for s in ("v", "a", "p", "t", "ldt", "lds", "ldr", "sn0", "sn1", "vc0", "vc1", "fx")])

@@ -2,18 +2,20 @@ from concourse.bass import DstId, RemoteDMATransfer
 from concourse.mybir import AluOpType as OP, ActivationFunctionType as AF
 
 M, K = 4096, 64
-H = M // 2
-FROW = [0, 2, 1, 3]
+MID = 1 << 23
 V_FILL = 5120
-P_FILL = 7168
+P_FILL = 1536
+HB = [0, 512, 2048, 3840]
+DIRECT = 1792
+W1 = 2048
 
 SCRATCH = {
     "fw": ("sbuf", [128, 4 * M], "bfloat16"),
     "sw": ("sbuf", [128, 4 * M], "bfloat16"),
     "vw": ("sbuf", [128, 4 * M], "bfloat16"),
-    "fl": ("dram", [4, 128, 1024], "bfloat16"),
+    "fl": ("dram", [12, 128, 256], "bfloat16"),
     "ta": ("sbuf", [128, 512], "int32"),
-    "ft": ("sbuf", [128, 1024], "bfloat16"),
+    "ft": ("sbuf", [128, 768], "bfloat16"),
     "sdi": ("sbuf", [128, 1], "int32"),
     "shi": ("sbuf", [128, 1], "int32"),
     "sdf": ("sbuf", [128, 1], "float32"),
@@ -22,13 +24,16 @@ SCRATCH = {
     "rkf": ("sbuf", [8, 8], "float32"),
     "f8": ("sbuf", [8, 128], "float32"),
     "gs": ("sbuf", [8, 128], "float32"),
-    "rkc": ("sbuf", [128, 8], "float32"),
     "a4": ("sbuf", [128, 4], "float32"),
-    "dj": ("sbuf", [128, 4], "float32"),
+    "bt": ("sbuf", [128, 4], "float32"),
+    "j1": ("sbuf", [128, 4], "float32"),
     "j4": ("sbuf", [128, 4], "float32"),
-    "ob": ("sbuf", [128, 128], "bfloat16"),
-    "cm": ("sbuf", [128, 2336], "bfloat16"),
+    "dl": ("sbuf", [128, 8], "float32"),
+    "am": ("sbuf", [128, 64], "int32"),
+    "cw": ("sbuf", [128, 64], "float32"),
+    "og": ("sbuf", [128, 448], "bfloat16"),
     "idt": ("sbuf", [128, 128], "bfloat16"),
+    "cm": ("sbuf", [128, 2208], "bfloat16"),
     "n1": ("sbuf", [128, 320], "int32"),
     "hx": ("sbuf", [128, 320], "int32"),
     "hl": ("sbuf", [128, 320], "int32"),
@@ -36,26 +41,18 @@ SCRATCH = {
     "hm": ("sbuf", [128, 320], "int32"),
     "hs2": ("sbuf", [128, 320], "int32"),
     "hb": ("sbuf", [128, 320], "int32"),
-    "ht": ("sbuf", [128, 320], "float32"),
     "ht2": ("sbuf", [128, 320], "int32"),
     "ha": ("sbuf", [128, 320], "int32"),
-    "of": ("sbuf", [128, 256], "float32"),
-    "oh": ("sbuf", [128, 256], "float32"),
-    "og": ("sbuf", [128, 192], "float32"),
-    "oge": ("sbuf", [128, 192], "float32"),
-    "op": ("sbuf", [128, 256], "float32"),
-    "o2": ("sbuf", [128, 128], "float32"),
-    "q4": ("sbuf", [128, 64], "float32"),
-    "q4b": ("sbuf", [128, 64], "bfloat16"),
+    "b4": ("sbuf", [128, 256], "float32"),
     "off": ("sbuf", [128, 256], "float32"),
     "l1": ("sbuf", [128, 256], "uint16"),
-    "l2": ("sbuf", [128, 256], "uint16"),
+    "l2": ("sbuf", [128, 192], "uint16"),
     "l3": ("sbuf", [128, 64], "uint16"),
     "acc": ("sbuf", [128, 256], "float32"),
-    "dd": ("sbuf", [128, 256], "float32"),
     "mm": ("sbuf", [128, 256], "float32"),
+    "xi": ("sbuf", [128, 256], "int32"),
+    "ai": ("sbuf", [128, 256], "int32"),
     "cc": ("sbuf", [128, 256], "float32"),
-    "dc": ("sbuf", [128, 192], "float32"),
     "vi": ("sbuf", [128, 64], "int32"),
     "vb": ("sbuf", [128, 64], "int32"),
     "mk": ("sbuf", [128, 192], "float32"),
@@ -63,16 +60,20 @@ SCRATCH = {
     "p2": ("sbuf", [128, 128], "float32"),
     "xx": ("sbuf", [128, 64], "float32"),
     "yt": ("sbuf", [128, 1024], "bfloat16"),
+    "on": ("sbuf", [128, 1024], "bfloat16"),
     "psr": ("psum", [128, 512], "float32"),
+    "psv": ("psum", [128, 512], "float32"),
+    "psq": ("psum", [128, 512], "float32"),
     "psk": ("psum", [128, 512], "float32"),
 }
 for _i in range(4):
     SCRATCH["ga%d" % _i] = ("sbuf", [128, 1024], "bfloat16")
-    SCRATCH["gb%d" % _i] = ("sbuf", [128, 1024], "bfloat16")
     SCRATCH["ps%d" % _i] = ("psum", [128, 512], "float32")
+for _i in range(3):
+    SCRATCH["gb%d" % _i] = ("sbuf", [128, 1024], "bfloat16")
 
-SEMAPHORES = ["v", "a", "p", "t", "ldt", "lds", "ldr", "sn0", "sn1", "vc0", "vc1", "fx", "st", "lr",
-              "aft0", "aft1", "aft2", "aft3", "asn", "avc", "hs1", "hv0", "hv1"]
+SEMAPHORES = ["v", "a", "p", "t", "ldt", "lds", "ldr", "sn0", "sn1", "sn2", "vc0", "vc1", "fx", "st", "lr",
+              "aft0", "aft1", "aft2", "aft3", "asn", "avc", "hs0", "hs1", "hs2", "hv0", "hv1"]
 
 
 def helper_of(core, T, topo):
@@ -94,18 +95,31 @@ def spread(g, T, topo, core, dsts, src, name, dst_ap):
     return len(topo.engines(core, dsts[0]))
 
 
+def after(T, r):
+    return [T.cores[(r + k) % len(T.cores)] for k in range(1, len(T.cores))]
+
+
+def hist(b):
+    return [(b + HB[j], b + HB[j + 1]) for j in range(len(HB) - 1)]
+
+
+def pieces(b):
+    m = (DIRECT + M) // 2
+    return [(b + DIRECT, b + m), (b + m, b + M)]
+
+
 def helper_program(g, core, T, topo, owner):
     r = T.rank_of(owner)
     ne = len(topo.engines(owner, core))
-    dsts = [c for c in T.cores if c != owner]
+    dsts = after(T, r)
     b = M * r
     n = 0
-    g.wait_ge(T.sem.hs1, ne)
-    n += spread(g, T, topo, core, dsts, T.sw[:, b + H:b + M], "asn", T.sw[:, b + H:b + M])
-    g.wait_ge(T.sem.hv0, ne)
-    n += spread(g, T, topo, core, dsts, T.vw[:, b:b + H], "avc", T.vw[:, b:b + H])
-    g.wait_ge(T.sem.hv1, ne)
-    n += spread(g, T, topo, core, dsts, T.vw[:, b + H:b + M], "avc", T.vw[:, b + H:b + M])
+    for j, (x0, x1) in enumerate(hist(b)):
+        g.wait_ge(T.sem["hs%d" % j], ne)
+        n += spread(g, T, topo, core, dsts, T.sw[:, x0:x1], "asn", T.sw[:, x0:x1])
+    for j, (x0, x1) in enumerate(pieces(b)):
+        g.wait_ge(T.sem["hv%d" % j], ne)
+        n += spread(g, T, topo, core, dsts, T.vw[:, x0:x1], "avc", T.vw[:, x0:x1])
     g.wait_ge(T.sem.lr, n)
 
 
@@ -117,8 +131,9 @@ def rank_program(g, core, T, topo):
                 helper_program(g, core, T, topo, c)
         return
 
-    others = [c for c in T.cores if c != core]
+    others = after(T, rank)
     hc = helper_of(core, T, topo)
+    ne = len(topo.engines(core, hc))
     b0 = M * rank
     engs = {"v": g.vector, "a": g.scalar, "p": g, "t": g.tensor, "s": g.sync}
     cnt = {}
@@ -155,47 +170,75 @@ def rank_program(g, core, T, topo):
     def FILL(ap, c):
         return done("v", v.memset(ap, c))
 
-    def dma(q, out, x, sem, *deps):
-        need(q, deps)
-        return done(q, engs[q].dma_start(out, x), 16, sem)
-
-    dma("s", T.ta[:, 0:256], T.thr[:, :], "ldt")
-    dma("s", T.sdi[:, :], T.sd[:, :], "lds")
-    ld_t = dma("a", T.ta[:, 256:512], T.ali[:, :], "ldt")
-    ld_r = dma("a", T.rki[:, :], T.rk[:, :], "ldr")
-    ld_s = ("lds", 16)
-    ld_s1 = dma("s", T.sw[:, b0 + H:b0 + M], T.seen[:, H:M], "sn1")
-    ld_s0 = dma("s", T.sw[:, b0:b0 + H], T.seen[:, 0:H], "sn0")
-    ld_v0 = dma("s", T.vw[:, b0:b0 + H], T.vec[:, 0:H], "vc0")
-    ld_v1 = dma("s", T.vw[:, b0 + H:b0 + M], T.vec[:, H:M], "vc1")
-
-    t_f8 = FILL(T.f8[:, :], 1.0)
-    t_ob = FILL(T.ob[:, :], 1.0)
-    t_f0 = FILL(T.fw[:, 0:2048], 1.0)
-    t_cm = FILL(T.cm[:, :], 0.0)
+    def COPY(out, x, scale, *deps):
+        need("a", deps)
+        return done("a", a.activation(out, x, AF.Copy, scale=scale))
 
     def SEL(out, x, pattern, op, base, ch, *deps):
         need("p", deps)
         return done("p", g.affine_select(out, x, pattern, op, 0.0, base, ch))
 
+    def CONST(out, pattern, c):
+        return done("p", g.iota(out, pattern, c, 0, allow_small_or_imprecise_dtypes=True))
+
+    def dma(q, out, x, sem, *deps):
+        need(q, deps)
+        return done(q, engs[q].dma_start(out, x), 16, sem)
+
+    def send(dsts, win, x0, x1, sem):
+        return spread(g, T, topo, core, dsts, win[:, x0:x1], sem, win[:, x0:x1])
+
+    def ld_seen(j, x0, x1):
+        return dma("s", T.sw[:, b0 + x0:b0 + x1], T.seen[:, x0:x1], "sn%d" % j)
+
+    ld_sn = [ld_seen(0, HB[0], HB[1])]
+    dma("a", T.ta[:, 0:256], T.thr[:, :], "ldt")
+    ld_t = dma("s", T.ta[:, 256:512], T.ali[:, :], "ldt")
+    ld_s = dma("a", T.sdi[:, :], T.sd[:, :], "lds")
+    ld_r = dma("a", T.rki[:, :], T.rk[:, :], "ldr")
+    ld_sn += [ld_seen(1, HB[1], HB[2]), ld_seen(2, HB[2], M)]
+
+    hp = hist(b0)
+    vp = pieces(b0)
+    t_f8 = FILL(T.f8[:, :], 1.0)
     t_gs = SEL(T.gs[:, :], T.f8[:, :], [[1, 128]], OP.is_ge, 0, -16, t_f8)
     t_gs = SEL(T.gs[:, :], T.gs[:, :], [[-1, 128]], OP.is_ge, 15, 16, t_gs)
-    t_n1 = done("p", g.iota(T.n1[:, :], [[1597, 5], [5 * 1597, 64]], -(1 << 23), 0))
-    t_j4 = done("p", g.iota(T.j4[:, :], [[M, 4]], 0, 0, allow_small_or_imprecise_dtypes=True))
-    mid = (V_FILL + P_FILL) // 2
-    t_pf0 = done("p", g.iota(T.fw[:, V_FILL:mid], [[0, mid - V_FILL]], 1, 0, allow_small_or_imprecise_dtypes=True))
+    lr = 0
+    for j in range(2):
+        need("p", [ld_sn[j]])
+        lr += send([hc], T.sw, hp[j][0], hp[j][1], "hs%d" % j)
+    t_n1 = done("p", g.iota(T.n1[:, :], [[1597, 5], [5 * 1597, 64]], -MID, 0))
 
-    fills = {}
-    need("a", [t_f0])
-    c0 = P_FILL
-    af = []
+    t_on = FILL(T.on[:, :], 1.0)
+    t_w0 = FILL(T.cm[:, W1:W1 + 144], 0.0)
+    regions = []
+
+    def blocks(x0, x1):
+        out = []
+        while x0 < x1:
+            e = min(x1, (x0 // M + 1) * M)
+            out.append((x0, e, (b0 + x0) % (4 * M)))
+            x0 = e
+        return out
+
+    for x0, x1, c in blocks(0, V_FILL):
+        regions.append((x0, x1, FILL(T.fw[:, c:c + x1 - x0], 1.0)))
+    c0 = V_FILL + P_FILL
     while c0 < 4 * M:
-        c1 = min(4 * M, (c0 // 2048 + 1) * 2048)
-        af.append((c0, c1, done("a", a.activation(T.fw[:, c0:c1], T.fw[:, 0:c1 - c0], AF.Copy))))
+        c1 = min(4 * M, (c0 // 1024 + 1) * 1024)
+        for y0, y1, c in blocks(c0, c1):
+            regions.append((y0, y1, COPY(T.fw[:, c:c + y1 - y0], T.on[:, 0:y1 - y0], 1.0, t_on)))
         c0 = c1
 
-    t_hi = CP(T.ft[:, 0:512], T.ta[:, :], ld_t)
-    t_ft = TT(T.ft[:, 512:1024], T.ta[:, :], T.ft[:, 0:512], OP.subtract, t_hi)
+    pk = T.psv[:, 0:256]
+    rp = T.psv[:, 256:512]
+    x = TS(pk, T.ta[:, 0:256], float(M), OP.mult, -float(MID), OP.add, ld_t)
+    x = TT(pk, pk, T.ta[:, 256:512], OP.add, x)
+    t_p = [None] * 3
+    t_p[0] = CP(T.ft[:, 0:256], pk, x)
+    x = TT(rp, pk, T.ft[:, 0:256], OP.subtract, t_p[0])
+    t_p[1] = CP(T.ft[:, 256:512], rp, x)
+    t_p[2] = TT(T.ft[:, 512:768], rp, T.ft[:, 256:512], OP.subtract, t_p[1])
 
     t_sdf = CP(T.sdf[:, :], T.sdi[:, :], ld_s)
     t_shi = TS(T.shi[:, :], T.sdi[:, :], 12, OP.logical_shift_right, None, None)
@@ -203,43 +246,46 @@ def rank_program(g, core, T, topo):
     t_cf = TS(T.cf[:, :], T.shi[:, :], 64.0, OP.mult, -float(1 << 22), OP.add, t_shi)
     need("t", [t_rkf, t_gs])
     t_psr = done("t", t.matmul(T.psr[:, 0:8], T.gs[:, :], T.rkf[:, :], True, True))
-    t_f1 = FILL(T.fw[:, 2048:V_FILL], 1.0)
 
-    need("p", [t_ft])
-    lr = spread(g, T, topo, core, others, T.ft[:, :], "aft%d" % rank, T.fl[rank])
-    need("p", [ld_s1])
-    lr += spread(g, T, topo, core, [hc], T.sw[:, b0 + H:b0 + M], "hs1", T.sw[:, b0 + H:b0 + M])
-    need("p", [ld_s0])
-    lr += spread(g, T, topo, core, others, T.sw[:, b0:b0 + H], "asn", T.sw[:, b0:b0 + H])
-    t_pf1 = done("p", g.iota(T.fw[:, mid:P_FILL], [[0, P_FILL - mid]], 1, 0, allow_small_or_imprecise_dtypes=True))
-    wt, wa = 2048, 2192
+    for f in range(3):
+        need("p", [t_p[f]])
+        lr += spread(g, T, topo, core, others, T.ft[:, 256 * f:256 * f + 256], "aft%d" % rank, T.fl[3 * rank + f])
+    t_j4 = CONST(T.j4[:, :], [[M, 4]], 0)
+    t_j1 = CONST(T.j1[:, :], [[M // 4, 4]], 0)
+    t_id = SEL(T.idt[:, :], T.on[:, 0:128], [[-1, 128]], OP.is_equal, 0, 1, t_on)
+    need("p", [ld_sn[2]])
+    lr += send([hc], T.sw, hp[2][0], hp[2][1], "hs2")
+    lr += send(others, T.sw, b0 + HB[3], b0 + M, "asn")
+    wm = T.cm[:, W1 + 15:W1 + 143:16]
+    t_w = SEL(wm, T.on[:, 0:8], [[-16, 8]], OP.is_ge, 0, 1, t_w0)
+    for y0, y1, c in blocks(V_FILL, V_FILL + P_FILL):
+        regions.append((y0, y1, CONST(T.fw[:, c:c + y1 - y0], [[0, y1 - y0]], 1)))
 
-    def diag(w, u):
-        return T.cm[:, w + 15 - u:w + 143 - u]
+    def diag(u):
+        return T.cm[:, W1 + 15 - u:W1 + 143 - u]
 
-    SEL(T.cm[:, wt + 15:wt + 143:16], T.ob[:, 0:8], [[-16, 8]], OP.is_ge, 0, 1, t_ob, t_cm)
-    t_w = SEL(T.cm[:, wa + 15:wa + 143:16], T.ob[:, 0:8], [[-16, 8]], OP.is_ge, -2, 1)
-    SEL(T.cm[:, wt + 15:wt + 143:16], T.cm[:, wt + 15:wt + 143:16], [[16, 8]], OP.is_ge, 1, -1, t_w)
-    SEL(T.cm[:, wa + 15:wa + 143:16], T.cm[:, wa + 15:wa + 143:16], [[16, 8]], OP.is_ge, 3, -1)
-    SEL(T.idt[:, :], T.ob[:, :], [[-1, 128]], OP.is_equal, 0, 1)
-    t_con = SEL(T.cm[:, 0:2048:16], T.ob[:, :], [[-1, 16], [-16, 8]], OP.is_equal, 0, 1)
-    ne = len(topo.engines(core, hc))
-    need("p", [ld_v0])
-    lr += spread(g, T, topo, core, [hc], T.vw[:, b0:b0 + H], "hv0", T.vw[:, b0:b0 + H])
-    need("p", [ld_v1])
-    lr += spread(g, T, topo, core, [hc], T.vw[:, b0 + H:b0 + M], "hv1", T.vw[:, b0 + H:b0 + M])
-
-    regions = [(0, 2048, t_f0), (2048, V_FILL, t_f1), (V_FILL, mid, t_pf0), (mid, P_FILL, t_pf1)] + af
-    t_fx = None
-    for q in range(4):
+    for k in range(4):
+        q = (rank + k) % 4
         lo, hi = M * q, M * q + M
-        deps = [tok for (x0, x1, tok) in regions if x0 < hi and lo < x1]
-        if q == 0:
-            deps += [af[-1][2]]
-        deps += [t_ft] if q == rank else [("aft%d" % q, len(topo.engines(T.cores[q], core)))]
-        for f in range(4):
-            x = T.ft[:, 256 * f:256 * f + 256] if q == rank else T.fl[q][:, 256 * f:256 * f + 256]
-            t_fx = dma("s", T.fw[FROW[f]::16, lo:hi], x, "fx", *deps)
+        deps = [tok for (x0, x1, tok) in regions if x0 < M * k + M and M * k < x1]
+        deps += [t_p[2]] if k == 0 else [("aft%d" % q, 3 * len(topo.engines(T.cores[q], core)))]
+        for f in range(3):
+            x = T.ft[:, 256 * f:256 * f + 256] if k == 0 else T.fl[3 * q + f]
+            t_fx = dma("s", T.fw[f::16, lo:hi], x, "fx", *deps)
+        if k == 0:
+            ld_v1 = dma("s", T.vw[:, b0 + DIRECT:b0 + M], T.vec[:, DIRECT:M], "vc1", t_w)
+    ld_v0 = dma("s", T.vw[:, b0:b0 + DIRECT], T.vec[:, 0:DIRECT], "vc0")
+
+    t_con1 = SEL(wm, wm, [[16, 8]], OP.is_ge, 2, -1, t_w)
+    CONST(T.cm[:, 0:512], [[0, 512]], 0)
+    need("p", [ld_v1])
+    for i in range(2):
+        lr += send([hc], T.vw, vp[i][0], vp[i][1], "hv%d" % i)
+    for j in range(1, 4):
+        x = CONST(T.cm[:, 512 * j:512 * j + 512], [[0, 512]], 0)
+    t_con = SEL(T.cm[:, 0:2048:16], T.on[:, 0:128], [[-1, 16], [-16, 8]], OP.is_equal, 0, 1, x)
+    need("p", [ld_v0])
+    lr += send(others, T.vw, b0, b0 + DIRECT, "avc")
 
     tok = {}
 
@@ -259,9 +305,9 @@ def rank_program(g, core, T, topo):
         elif s == 5:
             r = TS(T.hb[:, c], T.hs2[:, c], 6, OP.arith_shift_right, 4095, OP.bitwise_and, k(4))
         elif s == 6:
-            r = TT(T.ht[:, c], T.hb[:, c], T.hb[:, c], OP.mult, k(5))
+            r = TT(T.psv[:, c], T.hb[:, c], T.hb[:, c], OP.mult, k(5))
         elif s == 7:
-            r = TT(T.ht2[:, c], T.ht[:, c], T.hm[:, c], OP.add, k(6), k(3))
+            r = TT(T.ht2[:, c], T.psv[:, c], T.hm[:, c], OP.add, k(6), k(3))
         else:
             r = TS(T.ha[:, c], T.ht2[:, c], 6, OP.arith_shift_right, 4095, OP.bitwise_and, k(7))
         tok[(s, c0)] = r
@@ -270,129 +316,120 @@ def rank_program(g, core, T, topo):
     def O(s):
         return step(s, 0, 64)
 
-    def Ca(s):
-        return step(s, 64, 192)
+    def C(s):
+        return step(s, 64, 320)
 
-    def Cb(s):
-        return step(s, 192, 320)
-
-    O(0); Ca(0); O(1); Ca(1); O(2); Ca(2); O(3); O(4)
+    need("v", [t_p[2]])
+    O(0); C(0); O(1); C(1); O(2)
     t_a4 = TS(T.a4[:, :], T.psr[:, 4:8], float(M), OP.mult, None, None, t_psr)
-    t_rkc = CP(T.rkc[:, :], T.psr[:, 0:8])
+    O(3)
+    t_bt = TS(T.bt[:, :], T.psr[:, 0:4], 0.25, OP.mult, None, None)
+    O(4)
+    t_bt = TT(T.bt[:, :], T.bt[:, :], T.j1[:, :], OP.add, t_bt, t_j1)
+    TT(T.dl[:, 0:4], T.a4[:, :], T.j4[:, :], OP.subtract, t_j4, t_a4)
     O(5)
-    t_dj = TT(T.dj[:, :], T.j4[:, :], T.a4[:, :], OP.subtract, t_j4, t_a4)
-    Ca(3)
+    t_dl = TT(T.dl[:, 4:7], T.j4[:, 1:4], T.a4[:, 0:3], OP.subtract)
+    C(2)
     O(6)
-    for j in range(4):
-        tf = TS(T.of[:, 64 * j:64 * j + 64], T.hb[:, 0:64], T.rkc[:, j:j + 1], OP.is_lt, T.dj[:, j:j + 1], OP.mult, t_rkc, t_dj, tok[(5, 0)])
+    t_bq = TS(T.psq[:, 0:64], T.hb[:, 0:64], 0.25, OP.mult, None, None, tok[(5, 0)])
     O(7)
-    for j in range(4):
-        th = TS(T.oh[:, 64 * j:64 * j + 64], T.of[:, 64 * j:64 * j + 64], T.a4[:, j:j + 1], OP.add, None, None, tf)
-    O(8)
-    TS(T.op[:, 192:256], T.of[:, 0:64], T.a4[:, 0:1], OP.add, None, None)
-    tg = TT(T.og[:, :], T.oh[:, 64:256], T.oh[:, 0:192], OP.subtract, th)
-    for j in range(1, 4):
-        te = TS(T.oge[:, 64 * j - 64:64 * j], T.ha[:, 0:64], float(1024 * j), OP.is_ge, None, None, tok[(8, 0)])
-    Ca(4)
-    tp = TT(T.op[:, 0:192], T.oge[:, :], T.og[:, :], OP.mult, te, tg)
-    Ca(5)
-    tp = TT(T.o2[:, :], T.op[:, 0:128], T.op[:, 128:256], OP.add, tp)
-    Ca(6)
-    t_q4 = TT(T.q4[:, :], T.o2[:, 0:64], T.o2[:, 64:128], OP.add, tp)
-    Ca(7)
-    t_q4b = CP(T.q4b[:, :], T.q4[:, :], t_q4)
-    Ca(8)
+    C(3)
+    x = TS(T.am[:, :], T.ht2[:, 0:64], 6, OP.arith_shift_right, 3072, OP.bitwise_and, tok[(7, 0)])
+    x = TT(T.cw[:, :], T.am[:, :], T.psq[:, 0:64], OP.add, x, t_bq)
+    C(4)
+    for j in range(7):
+        lim = T.bt[:, j:j + 1] if j < 4 else float(1024 * (j - 3))
+        t_og = TS(T.og[:, 64 * j:64 * j + 64], T.cw[:, :], lim, OP.is_ge, T.dl[:, j:j + 1], OP.mult, x, t_bt, t_dl)
+    need("t", [t_og, t_id])
+    q4 = T.psr[:, 64:128]
+    for j in range(7):
+        ins = t.matmul(q4, T.idt[:, :], T.og[:, 64 * j:64 * j + 64], j == 0, j == 6)
+    t_q4 = done("t", ins)
+    C(5); C(6); C(7); C(8)
+    t_l1 = [None, None]
+    for h in range(2):
+        for i in (2 * h, 2 * h + 1):
+            x = TT(T.off[:, 64 * i:64 * i + 64], T.ha[:, 64 * i + 64:64 * i + 128], q4, OP.add, t_q4, tok[(8, 64)])
+        t_l1[h] = CP(T.l1[:, 128 * h:128 * h + 128], T.off[:, 128 * h:128 * h + 128], x)
+    t_b4 = TS(T.b4[:, :], T.hb[:, 64:320], float(M), OP.mult, float(M - 1 - MID), OP.add)
 
-    def offs(i):
-        return TT(T.off[:, 64 * i:64 * i + 64], T.ha[:, 64 * i + 64:64 * i + 128], T.q4[:, :], OP.add, t_q4,
-                  tok[(8, 64 if i < 2 else 192)])
-
-    Cb(0)
-    offs(0); x = offs(1)
-    Cb(1)
-    t_l1a = CP(T.l1[:, 0:128], T.off[:, 0:128], x)
-    Cb(2); Cb(3); Cb(4); Cb(5); Cb(6); Cb(7); Cb(8)
-    offs(2); x = offs(3)
-    t_l1b = CP(T.l1[:, 128:256], T.off[:, 128:256], x)
-
-    def gather_a(out, win, lst, scale, *deps):
-        need("a", deps)
-        return done("a", a.activation(out, win.indirect(lst), AF.Copy, scale=scale))
-
-    def gather_v(out, win, lst, scale, *deps):
-        need("v", deps)
+    def gather(q, out, win, lst, scale, *deps):
+        need(q, deps)
+        if q == "a":
+            return done("a", a.activation(out, win.indirect(lst), AF.Copy, scale=scale))
         if scale == 1.0:
             return done("v", v.tensor_copy(out, win.indirect(lst)))
         return done("v", v.tensor_scalar(out, win.indirect(lst), scale, None, OP.mult))
 
-    G = [None] * 4
-    G[0] = gather_a(T.ga0[:, :], T.fw[:, :], T.l1[:, 0:64], 1.0, t_fx, t_l1a)
-    G[1] = gather_a(T.ga1[:, :], T.fw[:, :], T.l1[:, 64:128], 1.0)
-    G[3] = gather_a(T.ga3[:, :], T.fw[:, :], T.l1[:, 192:256], 1.0, t_l1b)
-    G[2] = gather_v(T.ga2[:, :], T.fw[:, :], T.l1[:, 128:192], 1.0, t_fx, t_l1b)
+    G = [[], [], [], []]
+    E = [[], [], []]
+    d = [None] * 4
     PT = [None] * 4
-    for i in range(4):
-        need("t", [G[i], t_con, t_q4b])
-        src, ps = T["ga%d" % i], T["ps%d" % i]
+    all_s = ("asn", 3 * 4 * ne)
+
+    def GA(q, i, h0, h1):
+        G[i].append(gather(q, T["ga%d" % i][:, 512 * h0:512 * h1], T.fw[:, :], T.l1[:, 64 * i + 32 * h0:64 * i + 32 * h1], 1.0,
+                           t_fx, t_l1[i // 2]))
+
+    def PE(i):
+        need("t", G[i] + [t_con1])
         for u in range(16):
-            t.matmul(ps[:, 0:64], diag(wt, u), src[:, u::16], u == 0, u == 15)
-        for u in range(16):
-            t.matmul(ps[:, 64:128], diag(wa, u), src[:, u::16], u == 0, False)
-        PT[i] = done("t", t.matmul(ps[:, 64:128], T.idt[:, :], T.q4b[:, :], False, True))
+            ins = t.matmul(T["ps%d" % i][:, 0:64], diag(u), T["ga%d" % i][:, u::16], u == 0, u == 15)
+        PT[i] = done("t", ins)
 
-    def decide(pair):
-        tk = {}
-        for i in pair:
-            c, ps = slice(64 * i, 64 * i + 64), T["ps%d" % i]
-            TT(T.acc[:, c], ps[:, 0:64], T.hb[:, 64 * i + 64:64 * i + 128], OP.is_gt, PT[i])
-            tk[i] = TT(T.dd[:, c], T.off[:, c], ps[:, 64:128], OP.subtract)
-        for i in pair:
-            c = slice(64 * i, 64 * i + 64)
-            tk[i] = TT(T.mm[:, c], T.acc[:, c], T.dd[:, c], OP.mult, tk[i])
-        for i in pair:
-            c, ps = slice(64 * i, 64 * i + 64), T["ps%d" % i]
-            tk[i] = TT(T.cc[:, c], T.mm[:, c], ps[:, 64:128], OP.add, tk[i])
-        for i in pair:
-            c = slice(64 * i, 64 * i + 64)
-            tk[i] = CP(T.l2[:, c], T.cc[:, c], tk[i])
-        return tk
+    def decide(i):
+        c, ps = slice(64 * i, 64 * i + 64), T["ps%d" % i][:, 0:64]
+        x = TT(T.acc[:, c], ps, T.b4[:, c], OP.is_gt, PT[i], t_b4)
+        x = TT(T.psv[:, c], T.ha[:, 64 * i + 64:64 * i + 128], ps, OP.subtract) if False else TT(T.psv[:, c], T.ha[:, 64 * i + 64:64 * i + 128], ps, OP.subtract)
+        x = TT(T.mm[:, c], T.acc[:, c], T.psv[:, c], OP.mult, x)
+        x = TT(T.xi[:, c], T.mm[:, c], ps, OP.add, x)
+        x = TS(T.ai[:, c], T.xi[:, c], 4095, OP.bitwise_and, None, None, x)
+        x = TT(T.cc[:, c], T.ai[:, c], q4, OP.add, x)
+        d[i] = CP(T.l2[:, c], T.cc[:, c], x) if i < 3 else x
 
-    d01 = decide([0, 1])
-    d23 = decide([2, 3])
+    def HI(q, i, h0, h1):
+        E[i].append(gather(q, T["gb%d" % i][:, 512 * h0:512 * h1], T.sw[:, :], T.l2[:, 64 * i + 32 * h0:64 * i + 32 * h1],
+                           float(16 ** (2 - i)), all_s, ld_sn[0], ld_sn[1], ld_sn[2], d[i]))
 
-    all_s = ("asn", 3 * 2 * ne)
-    E = [[], [], [], []]
-    E[0].append(gather_a(T.gb0[:, :], T.sw[:, :], T.l2[:, 0:64], 4096.0, all_s, ld_s0, ld_s1, d01[0]))
-    E[1].append(gather_a(T.gb1[:, :], T.sw[:, :], T.l2[:, 64:128], 256.0, d01[1]))
-    E[2].append(gather_v(T.gb2[:, :], T.sw[:, :], T.l2[:, 128:192], 16.0, all_s, ld_s0, ld_s1, d23[2]))
-    E[3].append(gather_a(T.gb3[:, 0:512], T.sw[:, :], T.l2[:, 192:224], 1.0, d23[3]))
-    E[3].append(gather_v(T.gb3[:, 512:1024], T.sw[:, :], T.l2[:, 224:256], 1.0, d23[3]))
-    t_dc = TT(T.dc[:, :], T.cc[:, 64:256], T.cc[:, 0:192], OP.subtract)
+    for i in range(3):
+        GA("a", i, 0, 1)
+        GA("v", i, 1, 2)
+        PE(i)
+    GA("a", 3, 0, 1)
+    decide(0)
+    HI("a", 0, 0, 2)
+    decide(1)
+    GA("v", 3, 1, 2)
+    PE(3)
+    HI("a", 1, 0, 2)
+    decide(2)
+    HI("v", 2, 0, 1)
+    decide(3)
+    HI("v", 2, 1, 2)
+    dc = T.psq[:, 64:256]
+    t_dc = TT(dc, T.cc[:, 64:256], T.cc[:, 0:192], OP.subtract, d[3])
     CP(T.pp[:, 192:256], T.cc[:, 0:64])
-    t_psk = None
-    for i in range(4):
-        need("t", E[i])
-        src = T["gb%d" % i]
+    for i in range(3):
+        need("t", E[i] + [t_con])
         for u in range(16):
-            ins = t.matmul(T.psk[:, 0:64], T.cm[:, 127 * u:127 * u + 128], src[:, u::16], i + u == 0, i == 3 and u == 15)
+            ins = t.matmul(T.psk[:, 0:64], T.cm[:, 127 * u:127 * u + 128], T["gb%d" % i][:, u::16], i + u == 0, i == 2 and u == 15)
     t_psk = done("t", ins)
 
     x = CP(T.vi[:, :], T.psk[:, 0:64], t_psk)
-    x = TS(T.vb[:, :], T.vi[:, :], rank, OP.logical_shift_right, 0x1111, OP.bitwise_and, x)
-    y = None
-    for j, lim in enumerate((0x1000, 0x1100, 0x1110)):
+    x = TS(T.vb[:, :], T.vi[:, :], rank, OP.logical_shift_right, 0x111, OP.bitwise_and, x)
+    for j, lim in enumerate((0x100, 0x110, 0x111)):
         y = TS(T.mk[:, 64 * j:64 * j + 64], T.vb[:, :], float(lim), OP.is_ge, None, None, x)
-    x = TT(T.pp[:, 0:192], T.mk[:, :], T.dc[:, :], OP.mult, y, t_dc)
+    x = TT(T.pp[:, 0:192], T.mk[:, :], dc, OP.mult, y, t_dc)
     x = TT(T.p2[:, :], T.pp[:, 0:128], T.pp[:, 128:256], OP.add, x)
     t_x = TT(T.xx[:, :], T.p2[:, 0:64], T.p2[:, 64:128], OP.add, x)
     t_l3 = CP(T.l3[:, :], T.xx[:, :], t_x)
     dma("s", T.chosen[:, :], T.xx[:, :], "st", t_x)
 
-    all_v = ("avc", 3 * 2 * ne)
-    ya = gather_a(T.yt[:, 512:1024], T.vw[:, :], T.l3[:, 32:64], 1.0, all_v, ld_v0, ld_v1, t_l3)
-    yv = gather_v(T.yt[:, 0:512], T.vw[:, :], T.l3[:, 0:32], 1.0, all_v, ld_v0, ld_v1, t_l3)
+    all_v = ("avc", 3 * 3 * ne)
+    ya = gather("a", T.yt[:, 512:1024], T.vw[:, :], T.l3[:, 32:64], 1.0, all_v, ld_v0, ld_v1, t_l3)
+    yv = gather("v", T.yt[:, 0:512], T.vw[:, :], T.l3[:, 0:32], 1.0, all_v, ld_v0, ld_v1, t_l3)
     dma("s", T.y[:, 0:512], T.yt[:, 0:512], "st", yv)
     t_st = dma("a", T.y[:, 512:1024], T.yt[:, 512:1024], "st", ya)
 
     need("p", [("lr", lr)])
-    need("s", [t_st] + [(s, cnt[s]) for s in ("v", "a", "p", "t", "ldt", "lds", "ldr", "sn0", "sn1", "vc0", "vc1", "fx")])
+    need("s", [t_st] + [(s, cnt[s]) for s in ("v", "a", "p", "t", "ldt", "lds", "ldr", "sn0", "sn1", "sn2", "vc0", "vc1", "fx")])

@@ -2,16 +2,26 @@ from concourse.bass import DstId, RemoteDMATransfer
 from concourse.mybir import AluOpType as OP, ActivationFunctionType as AF
 
 M, K = 4096, 64
-MID = 1 << 23
-V_FILL = 5120
-P_FILL = 1536
-HB = [0, 512, 2048, 3840]
-DIRECT = 1792
+H = M // 2
+MID = 1 << 24
+N1 = 1 << 23
+V_FILL = 5632
+P_FILL = 1024
+SRC = 1024
+HP = [0, 256, 1280, 2048]
+PP = [(0, 256, "psq", 0), (256, 768, "ps0", 1), (768, 1280, "ps1", 1), (1280, 1792, "ps2", 2), (1792, 2048, "ps3", 2)]
+A_FILLS = [4, 2, 1, 1, 0]
+VP = [(0, 896, 1), (896, 1792, 1), (1792, 4096, 0)]
+P_ORDER = ["h0", "t0", "t1", "t2", "fill", "w", "h1", "h2", "v0", "v1", "con", "v2"]
+S_ORDER = ["f0", "f1", "f2", "f3", "v0", "v1", "v2"]
+G3 = 48
+HA = [56, 40, 32]
 W1 = 2048
 
 SCRATCH = {
     "fw": ("sbuf", [128, 4 * M], "bfloat16"),
-    "sw": ("sbuf", [128, 4 * M], "bfloat16"),
+    "sr": ("sbuf", [128, M], "bfloat16"),
+    "sw": ("sbuf", [128, 4 * H], "bfloat16"),
     "vw": ("sbuf", [128, 4 * M], "bfloat16"),
     "fl": ("dram", [12, 128, 256], "bfloat16"),
     "ta": ("sbuf", [128, 512], "int32"),
@@ -33,6 +43,7 @@ SCRATCH = {
     "cw": ("sbuf", [128, 64], "float32"),
     "og": ("sbuf", [128, 448], "bfloat16"),
     "idt": ("sbuf", [128, 128], "bfloat16"),
+    "id16": ("sbuf", [128, 128], "bfloat16"),
     "cm": ("sbuf", [128, 2208], "bfloat16"),
     "n1": ("sbuf", [128, 320], "int32"),
     "hx": ("sbuf", [128, 320], "int32"),
@@ -43,24 +54,24 @@ SCRATCH = {
     "hb": ("sbuf", [128, 320], "int32"),
     "ht2": ("sbuf", [128, 320], "int32"),
     "ha": ("sbuf", [128, 320], "int32"),
-    "b4": ("sbuf", [128, 256], "float32"),
+    "ce": ("sbuf", [128, 256], "float32"),
     "off": ("sbuf", [128, 256], "float32"),
     "l1": ("sbuf", [128, 256], "uint16"),
     "l2": ("sbuf", [128, 192], "uint16"),
     "l3": ("sbuf", [128, 64], "uint16"),
-    "acc": ("sbuf", [128, 256], "float32"),
-    "mm": ("sbuf", [128, 256], "float32"),
     "xi": ("sbuf", [128, 256], "int32"),
+    "ah": ("sbuf", [128, 192], "int32"),
+    "lh": ("sbuf", [128, 192], "float32"),
     "ai": ("sbuf", [128, 256], "int32"),
+    "mh": ("sbuf", [128, 192], "float32"),
     "cc": ("sbuf", [128, 256], "float32"),
-    "vi": ("sbuf", [128, 64], "int32"),
-    "vb": ("sbuf", [128, 64], "int32"),
-    "mk": ("sbuf", [128, 192], "float32"),
-    "pp": ("sbuf", [128, 256], "float32"),
-    "p2": ("sbuf", [128, 128], "float32"),
+    "vi": ("sbuf", [128, 192], "int32"),
+    "vb": ("sbuf", [128, 192], "int32"),
+    "uu": ("sbuf", [128, 192], "float32"),
     "xx": ("sbuf", [128, 64], "float32"),
     "yt": ("sbuf", [128, 1024], "bfloat16"),
-    "on": ("sbuf", [128, 1024], "bfloat16"),
+    "on": ("sbuf", [128, 128], "bfloat16"),
+    "o16": ("sbuf", [128, 128], "bfloat16"),
     "psr": ("psum", [128, 512], "float32"),
     "psv": ("psum", [128, 512], "float32"),
     "psq": ("psum", [128, 512], "float32"),
@@ -72,8 +83,8 @@ for _i in range(4):
 for _i in range(3):
     SCRATCH["gb%d" % _i] = ("sbuf", [128, 1024], "bfloat16")
 
-SEMAPHORES = ["v", "a", "p", "t", "ldt", "lds", "ldr", "sn0", "sn1", "sn2", "vc0", "vc1", "fx", "st", "lr",
-              "aft0", "aft1", "aft2", "aft3", "asn", "avc", "hs0", "hs1", "hs2", "hv0", "hv1"]
+SEMAPHORES = ["v", "a", "p", "t", "ldt", "lds", "ldr", "fx", "st", "lr", "aft0", "aft1", "aft2", "aft3", "asn", "avc"]
+SEMAPHORES += ["%s%d" % (s, j) for s in ("sn", "hs", "vc", "hv") for j in range(6)]
 
 
 def helper_of(core, T, topo):
@@ -100,24 +111,24 @@ def after(T, r):
 
 
 def hist(b):
-    return [(b + HB[j], b + HB[j + 1]) for j in range(len(HB) - 1)]
+    return [(b + HP[j], b + HP[j + 1]) for j in range(len(HP) - 1)]
 
 
 def pieces(b):
-    m = (DIRECT + M) // 2
-    return [(b + DIRECT, b + m), (b + m, b + M)]
+    return [(b + x0, b + x1, by) for x0, x1, by in VP]
 
 
 def helper_program(g, core, T, topo, owner):
     r = T.rank_of(owner)
     ne = len(topo.engines(owner, core))
     dsts = after(T, r)
-    b = M * r
     n = 0
-    for j, (x0, x1) in enumerate(hist(b)):
+    for j, (x0, x1) in enumerate(hist(H * r)):
         g.wait_ge(T.sem["hs%d" % j], ne)
         n += spread(g, T, topo, core, dsts, T.sw[:, x0:x1], "asn", T.sw[:, x0:x1])
-    for j, (x0, x1) in enumerate(pieces(b)):
+    for j, (x0, x1, by) in enumerate(pieces(M * r)):
+        if not by:
+            continue
         g.wait_ge(T.sem["hv%d" % j], ne)
         n += spread(g, T, topo, core, dsts, T.vw[:, x0:x1], "avc", T.vw[:, x0:x1])
     g.wait_ge(T.sem.lr, n)
@@ -138,6 +149,7 @@ def rank_program(g, core, T, topo):
     engs = {"v": g.vector, "a": g.scalar, "p": g, "t": g.tensor, "s": g.sync}
     cnt = {}
     seen = {k: {} for k in engs}
+    tok = {}
 
     def need(q, toks):
         for name, val in toks:
@@ -188,106 +200,47 @@ def rank_program(g, core, T, topo):
     def send(dsts, win, x0, x1, sem):
         return spread(g, T, topo, core, dsts, win[:, x0:x1], sem, win[:, x0:x1])
 
-    def ld_seen(j, x0, x1):
-        return dma("s", T.sw[:, b0 + x0:b0 + x1], T.seen[:, x0:x1], "sn%d" % j)
+    def ld_seen(j):
+        for x in (0, H):
+            r = dma("s", T.sr[:, x + HP[j]:x + HP[j + 1]], T.seen[:, x + HP[j]:x + HP[j + 1]], "sn%d" % j)
+        return r
 
-    ld_sn = [ld_seen(0, HB[0], HB[1])]
-    dma("a", T.ta[:, 0:256], T.thr[:, :], "ldt")
-    ld_t = dma("s", T.ta[:, 256:512], T.ali[:, :], "ldt")
     ld_s = dma("a", T.sdi[:, :], T.sd[:, :], "lds")
+    dma("s", T.ta[:, 256:512], T.ali[:, :], "ldt")
+    ld_t = dma("a", T.ta[:, 0:256], T.thr[:, :], "ldt")
     ld_r = dma("a", T.rki[:, :], T.rk[:, :], "ldr")
-    ld_sn += [ld_seen(1, HB[1], HB[2]), ld_seen(2, HB[2], M)]
+    ld_sn = [ld_seen(j) for j in range(len(HP) - 1)]
 
-    hp = hist(b0)
-    vp = pieces(b0)
-    t_f8 = FILL(T.f8[:, :], 1.0)
-    t_gs = SEL(T.gs[:, :], T.f8[:, :], [[1, 128]], OP.is_ge, 0, -16, t_f8)
-    t_gs = SEL(T.gs[:, :], T.gs[:, :], [[-1, 128]], OP.is_ge, 15, 16, t_gs)
-    lr = 0
-    for j in range(2):
-        need("p", [ld_sn[j]])
-        lr += send([hc], T.sw, hp[j][0], hp[j][1], "hs%d" % j)
-    t_n1 = done("p", g.iota(T.n1[:, :], [[1597, 5], [5 * 1597, 64]], -MID, 0))
-
-    t_on = FILL(T.on[:, :], 1.0)
-    t_w0 = FILL(T.cm[:, W1:W1 + 144], 0.0)
     regions = []
+
+    def col(x):
+        return (b0 + x) % (4 * M)
 
     def blocks(x0, x1):
         out = []
         while x0 < x1:
             e = min(x1, (x0 // M + 1) * M)
-            out.append((x0, e, (b0 + x0) % (4 * M)))
+            out.append((x0, e, col(x0)))
             x0 = e
         return out
 
+    cs = col(4 * M - SRC)
+    t_on = FILL(T.on[:, :], 1.0)
+    t_o16 = FILL(T.o16[:, :], 16.0)
+    t_src = FILL(T.fw[:, cs:cs + SRC], 1.0)
+    regions.append((4 * M - SRC, 4 * M, t_src))
+    t_f8 = FILL(T.f8[:, :], 1.0)
+    t_w0 = FILL(T.cm[:, W1:W1 + 144], 0.0)
     for x0, x1, c in blocks(0, V_FILL):
         regions.append((x0, x1, FILL(T.fw[:, c:c + x1 - x0], 1.0)))
-    c0 = V_FILL + P_FILL
-    while c0 < 4 * M:
-        c1 = min(4 * M, (c0 // 1024 + 1) * 1024)
-        for y0, y1, c in blocks(c0, c1):
-            regions.append((y0, y1, COPY(T.fw[:, c:c + y1 - y0], T.on[:, 0:y1 - y0], 1.0, t_on)))
-        c0 = c1
 
-    pk = T.psv[:, 0:256]
-    rp = T.psv[:, 256:512]
-    x = TS(pk, T.ta[:, 0:256], float(M), OP.mult, -float(MID), OP.add, ld_t)
-    x = TT(pk, pk, T.ta[:, 256:512], OP.add, x)
-    t_p = [None] * 3
-    t_p[0] = CP(T.ft[:, 0:256], pk, x)
-    x = TT(rp, pk, T.ft[:, 0:256], OP.subtract, t_p[0])
-    t_p[1] = CP(T.ft[:, 256:512], rp, x)
-    t_p[2] = TT(T.ft[:, 512:768], rp, T.ft[:, 256:512], OP.subtract, t_p[1])
-
-    t_sdf = CP(T.sdf[:, :], T.sdi[:, :], ld_s)
-    t_shi = TS(T.shi[:, :], T.sdi[:, :], 12, OP.logical_shift_right, None, None)
-    t_rkf = CP(T.rkf[:, :], T.rki[:, :], ld_r)
-    t_cf = TS(T.cf[:, :], T.shi[:, :], 64.0, OP.mult, -float(1 << 22), OP.add, t_shi)
-    need("t", [t_rkf, t_gs])
-    t_psr = done("t", t.matmul(T.psr[:, 0:8], T.gs[:, :], T.rkf[:, :], True, True))
-
-    for f in range(3):
-        need("p", [t_p[f]])
-        lr += spread(g, T, topo, core, others, T.ft[:, 256 * f:256 * f + 256], "aft%d" % rank, T.fl[3 * rank + f])
+    t_id = SEL(T.idt[:, :], T.on[:, :], [[-1, 128]], OP.is_equal, 0, 1, t_on)
+    t_id6 = SEL(T.id16[:, :], T.o16[:, :], [[-1, 128]], OP.is_equal, 0, 1, t_o16)
+    t_n1 = done("p", g.iota(T.n1[:, :], [[1597, 5], [5 * 1597, 64]], -N1, 0))
+    t_gs = SEL(T.gs[:, :], T.f8[:, :], [[1, 128]], OP.is_ge, 0, -16, t_f8)
+    t_gs = SEL(T.gs[:, :], T.gs[:, :], [[-1, 128]], OP.is_ge, 15, 16, t_gs)
     t_j4 = CONST(T.j4[:, :], [[M, 4]], 0)
     t_j1 = CONST(T.j1[:, :], [[M // 4, 4]], 0)
-    t_id = SEL(T.idt[:, :], T.on[:, 0:128], [[-1, 128]], OP.is_equal, 0, 1, t_on)
-    need("p", [ld_sn[2]])
-    lr += send([hc], T.sw, hp[2][0], hp[2][1], "hs2")
-    lr += send(others, T.sw, b0 + HB[3], b0 + M, "asn")
-    wm = T.cm[:, W1 + 15:W1 + 143:16]
-    t_w = SEL(wm, T.on[:, 0:8], [[-16, 8]], OP.is_ge, 0, 1, t_w0)
-    for y0, y1, c in blocks(V_FILL, V_FILL + P_FILL):
-        regions.append((y0, y1, CONST(T.fw[:, c:c + y1 - y0], [[0, y1 - y0]], 1)))
-
-    def diag(u):
-        return T.cm[:, W1 + 15 - u:W1 + 143 - u]
-
-    for k in range(4):
-        q = (rank + k) % 4
-        lo, hi = M * q, M * q + M
-        deps = [tok for (x0, x1, tok) in regions if x0 < M * k + M and M * k < x1]
-        deps += [t_p[2]] if k == 0 else [("aft%d" % q, 3 * len(topo.engines(T.cores[q], core)))]
-        for f in range(3):
-            x = T.ft[:, 256 * f:256 * f + 256] if k == 0 else T.fl[3 * q + f]
-            t_fx = dma("s", T.fw[f::16, lo:hi], x, "fx", *deps)
-        if k == 0:
-            ld_v1 = dma("s", T.vw[:, b0 + DIRECT:b0 + M], T.vec[:, DIRECT:M], "vc1", t_w)
-    ld_v0 = dma("s", T.vw[:, b0:b0 + DIRECT], T.vec[:, 0:DIRECT], "vc0")
-
-    t_con1 = SEL(wm, wm, [[16, 8]], OP.is_ge, 2, -1, t_w)
-    CONST(T.cm[:, 0:512], [[0, 512]], 0)
-    need("p", [ld_v1])
-    for i in range(2):
-        lr += send([hc], T.vw, vp[i][0], vp[i][1], "hv%d" % i)
-    for j in range(1, 4):
-        x = CONST(T.cm[:, 512 * j:512 * j + 512], [[0, 512]], 0)
-    t_con = SEL(T.cm[:, 0:2048:16], T.on[:, 0:128], [[-1, 16], [-16, 8]], OP.is_equal, 0, 1, x)
-    need("p", [ld_v0])
-    lr += send(others, T.vw, b0, b0 + DIRECT, "avc")
-
-    tok = {}
 
     def step(s, c0, c1):
         c = slice(c0, c1)
@@ -305,9 +258,9 @@ def rank_program(g, core, T, topo):
         elif s == 5:
             r = TS(T.hb[:, c], T.hs2[:, c], 6, OP.arith_shift_right, 4095, OP.bitwise_and, k(4))
         elif s == 6:
-            r = TT(T.psv[:, c], T.hb[:, c], T.hb[:, c], OP.mult, k(5))
+            r = TT(T.psk[:, c], T.hb[:, c], T.hb[:, c], OP.mult, k(5))
         elif s == 7:
-            r = TT(T.ht2[:, c], T.psv[:, c], T.hm[:, c], OP.add, k(6), k(3))
+            r = TT(T.ht2[:, c], T.psk[:, c], T.hm[:, c], OP.add, k(6), k(3))
         else:
             r = TS(T.ha[:, c], T.ht2[:, c], 6, OP.arith_shift_right, 4095, OP.bitwise_and, k(7))
         tok[(s, c0)] = r
@@ -316,120 +269,315 @@ def rank_program(g, core, T, topo):
     def O(s):
         return step(s, 0, 64)
 
-    def C(s):
-        return step(s, 64, 320)
+    def X(s):
+        return step(s, 64, 192)
 
-    need("v", [t_p[2]])
-    O(0); C(0); O(1); C(1); O(2)
-    t_a4 = TS(T.a4[:, :], T.psr[:, 4:8], float(M), OP.mult, None, None, t_psr)
+    def Y(s):
+        return step(s, 192, 320)
+
+    pk = T.psv[:, 0:256]
+    rp = T.psv[:, 256:512]
+    t_p = [None] * 3
+    t_sdf = CP(T.sdf[:, :], T.sdi[:, :], ld_s)
+    t_shi = TS(T.shi[:, :], T.sdi[:, :], 12, OP.logical_shift_right, None, None)
+    x = TS(pk, T.ta[:, 0:256], float(2 * M), OP.mult, -float(MID), OP.add, ld_t)
+    t_cf = TS(T.cf[:, :], T.shi[:, :], 64.0, OP.mult, -float(1 << 22), OP.add, t_shi)
+    O(0)
+    x = TT(pk, pk, T.ta[:, 256:512], OP.add, x)
+    t_rkf = CP(T.rkf[:, :], T.rki[:, :], ld_r)
+    O(1)
+    t_p[0] = CP(T.ft[:, 0:256], pk, x)
+    X(0)
+    x = TT(rp, pk, T.ft[:, 0:256], OP.subtract, t_p[0])
+    Y(0)
+    t_p[1] = CP(T.ft[:, 256:512], rp, x)
+    O(2)
     O(3)
-    t_bt = TS(T.bt[:, :], T.psr[:, 0:4], 0.25, OP.mult, None, None)
-    O(4)
-    t_bt = TT(T.bt[:, :], T.bt[:, :], T.j1[:, :], OP.add, t_bt, t_j1)
-    TT(T.dl[:, 0:4], T.a4[:, :], T.j4[:, :], OP.subtract, t_j4, t_a4)
-    O(5)
-    t_dl = TT(T.dl[:, 4:7], T.j4[:, 1:4], T.a4[:, 0:3], OP.subtract)
-    C(2)
-    O(6)
-    t_bq = TS(T.psq[:, 0:64], T.hb[:, 0:64], 0.25, OP.mult, None, None, tok[(5, 0)])
-    O(7)
-    C(3)
-    x = TS(T.am[:, :], T.ht2[:, 0:64], 6, OP.arith_shift_right, 3072, OP.bitwise_and, tok[(7, 0)])
-    x = TT(T.cw[:, :], T.am[:, :], T.psq[:, 0:64], OP.add, x, t_bq)
-    C(4)
-    for j in range(7):
+    t_p[2] = TT(T.ft[:, 512:768], rp, T.ft[:, 256:512], OP.subtract, t_p[1])
+
+    fills = []
+    c0 = V_FILL + P_FILL
+    while c0 < 4 * M - SRC:
+        c1 = min(4 * M - SRC, (c0 // 1024 + 1) * 1024)
+        fills.append((c0, c1))
+        c0 = c1
+
+    def a_fill(n):
+        for c0, c1 in fills[:n]:
+            c = col(c0)
+            regions.append((c0, c1, COPY(T.fw[:, c:c + c1 - c0], T.fw[:, cs:cs + c1 - c0], 1.0, t_src)))
+        del fills[:n]
+
+    t_ev = []
+    for j, (x0, x1, bank, grp) in enumerate(PP):
+        ps = T[bank][:, 0:x1 - x0]
+        need("t", [ld_sn[grp], t_id, t_id6])
+        t.matmul(ps, T.idt[:, :], T.sr[:, x0:x1], True, False)
+        x = done("t", t.matmul(ps, T.id16[:, :], T.sr[:, H + x0:H + x1], False, True))
+        if j == 0:
+            need("t", [t_rkf, t_gs])
+            t_psr = done("t", t.matmul(T.psr[:, 0:8], T.gs[:, :], T.rkf[:, :], True, True))
+        a_fill(A_FILLS[j])
+        t_ev.append(COPY(T.sw[:, H * rank + x0:H * rank + x1], ps, 1.0, x))
+    a_fill(len(fills))
+    for j in range(2):
+        t_zero = COPY(T.cm[:, 1024 * j:1024 * j + 1024], T.sr[:, 0:1024], 0.0, *ld_sn)
+
+    hp = hist(H * rank)
+    vp = pieces(b0)
+    ld_v = [None] * len(vp)
+
+    def s_vec(j):
+        x0, x1, by = vp[j]
+        ld_v[j] = dma("s", T.vw[:, x0:x1], T.vec[:, x0 - b0:x1 - b0], "vc%d" % j)
+
+    def s_parts(k):
+        q = (rank + k) % 4
+        lo, hi = M * q, M * q + M
+        deps = [tk for (x0, x1, tk) in regions if x0 < M * k + M and M * k < x1]
+        deps += [t_p[2]] if k == 0 else [("aft%d" % q, 3 * len(topo.engines(T.cores[q], core)))]
+        for f in range(3):
+            x = T.ft[:, 256 * f:256 * f + 256] if k == 0 else T.fl[3 * q + f]
+            tok["fx"] = dma("s", T.fw[f::16, lo:hi], x, "fx", *deps)
+
+    wm = T.cm[:, W1 + 15:W1 + 143:16]
+    lr = [0]
+
+    def p_hist(j):
+        need("p", [t_ev[i] for i in range(len(PP)) if PP[i][3] == j])
+        lr[0] += send([hc], T.sw, hp[j][0], hp[j][1], "hs%d" % j)
+
+    def p_part(f):
+        need("p", [t_p[f]])
+        lr[0] += spread(g, T, topo, core, others, T.ft[:, 256 * f:256 * f + 256], "aft%d" % rank, T.fl[3 * rank + f])
+
+    def p_vec(j):
+        x0, x1, by = vp[j]
+        need("p", [ld_v[j]])
+        lr[0] += send([hc] if by else others, T.vw, x0, x1, "hv%d" % j if by else "avc")
+
+    def p_fill(j):
+        for y0, y1, c in blocks(V_FILL, V_FILL + P_FILL):
+            regions.append((y0, y1, CONST(T.fw[:, c:c + y1 - y0], [[0, y1 - y0]], 1)))
+
+    def p_w(j):
+        x = SEL(wm, T.on[:, 0:8], [[-16, 8]], OP.is_ge, 0, 1, t_w0)
+        tok["w"] = SEL(wm, wm, [[16, 8]], OP.is_ge, 2, -1, x)
+
+    def p_con(j):
+        tok["con"] = SEL(T.cm[:, 0:2048:16], T.o16[:, :], [[-1, 16], [-16, 8]], OP.is_equal, 0, 1, t_zero)
+
+    calls = {"h": p_hist, "t": p_part, "v": p_vec, "fill": p_fill, "w": p_w, "con": p_con, "f": s_parts}
+
+    def call(n):
+        if n in calls:
+            calls[n](0)
+        else:
+            calls[n[0]](int(n[1:]))
+
+    todo = list(S_ORDER)
+
+    def s_next():
+        n = todo.pop(0)
+        if n[0] == "v":
+            s_vec(int(n[1:]))
+        else:
+            call(n)
+
+    for n in P_ORDER:
+        while n[0] == "v" and ld_v[int(n[1:])] is None:
+            s_next()
+        call(n)
+    while todo:
+        s_next()
+
+    def diag(u):
+        return T.cm[:, W1 + 15 - u:W1 + 143 - u]
+
+    def bt0():
+        tok["bt"] = TS(T.bt[:, :], T.psr[:, 0:4], 0.25, OP.mult, None, None, t_psr)
+
+    def a40():
+        tok["a4"] = TS(T.a4[:, :], T.psr[:, 4:8], float(M), OP.mult, None, None, t_psr)
+
+    def bt1():
+        tok["bt"] = TT(T.bt[:, :], T.bt[:, :], T.j1[:, :], OP.add, tok["bt"], t_j1)
+
+    def dl0():
+        TT(T.dl[:, 0:4], T.a4[:, :], T.j4[:, :], OP.subtract, tok["a4"], t_j4)
+        tok["dl"] = TT(T.dl[:, 4:7], T.j4[:, 1:4], T.a4[:, 0:3], OP.subtract)
+
+    def bq():
+        tok["bq"] = TS(T.psq[:, 0:64], T.hb[:, 0:64], 0.25, OP.mult, None, None, tok[(5, 0)], t_ev[0])
+
+    def am():
+        tok["am"] = TS(T.am[:, :], T.ht2[:, 0:64], 6, OP.arith_shift_right, 3072, OP.bitwise_and, tok[(7, 0)])
+
+    def cw():
+        tok["cw"] = TT(T.cw[:, :], T.am[:, :], T.psq[:, 0:64], OP.add, tok["am"], tok["bq"])
+
+    def og(j):
         lim = T.bt[:, j:j + 1] if j < 4 else float(1024 * (j - 3))
-        t_og = TS(T.og[:, 64 * j:64 * j + 64], T.cw[:, :], lim, OP.is_ge, T.dl[:, j:j + 1], OP.mult, x, t_bt, t_dl)
-    need("t", [t_og, t_id])
+        tok["og"] = TS(T.og[:, 64 * j:64 * j + 64], T.cw[:, :], lim, OP.is_ge, T.dl[:, j:j + 1], OP.mult,
+                       tok["cw"], tok["bt"], tok["dl"])
+
+    own = [lambda: O(4), bt0, lambda: O(5), a40, lambda: O(6), bq, lambda: O(7), bt1, am, dl0, cw]
+    own += [lambda j=j: og(j) for j in range(7)]
+    cand = [lambda f=f, s=s: f(s) for s in range(1, 9) for f in (X, Y)]
+    while own or cand:
+        if own:
+            own.pop(0)()
+        if cand:
+            cand.pop(0)()
     q4 = T.psr[:, 64:128]
+    q2 = T.psr[:, 128:192]
+    need("t", [tok["og"], t_id])
     for j in range(7):
         ins = t.matmul(q4, T.idt[:, :], T.og[:, 64 * j:64 * j + 64], j == 0, j == 6)
     t_q4 = done("t", ins)
-    C(5); C(6); C(7); C(8)
+    cb = T.psq[:, 128:384]
+    x = TS(cb, T.hb[:, 64:320], float(2 * M), OP.mult, float(M - MID), OP.add)
+    t_ce = TT(T.ce[:, :], cb, T.ha[:, 64:320], OP.add, x, tok[(8, 64)], tok[(8, 192)])
+    x = [None] * 4
     t_l1 = [None, None]
-    for h in range(2):
-        for i in (2 * h, 2 * h + 1):
-            x = TT(T.off[:, 64 * i:64 * i + 64], T.ha[:, 64 * i + 64:64 * i + 128], q4, OP.add, t_q4, tok[(8, 64)])
-        t_l1[h] = CP(T.l1[:, 128 * h:128 * h + 128], T.off[:, 128 * h:128 * h + 128], x)
-    t_b4 = TS(T.b4[:, :], T.hb[:, 64:320], float(M), OP.mult, float(M - 1 - MID), OP.add)
+    for i in range(4):
+        x[i] = TT(T.off[:, 64 * i:64 * i + 64], T.ha[:, 64 * i + 64:64 * i + 128], q4, OP.add, t_q4)
+        if i >= 2:
+            h = i - 2
+            t_l1[h] = CP(T.l1[:, 128 * h:128 * h + 128], T.off[:, 128 * h:128 * h + 128], x[2 * h + 1])
+    t_q2 = TS(q2, q4, 0.5, OP.mult, None, None)
 
-    def gather(q, out, win, lst, scale, *deps):
+    def gather(q, out, win, lst, *deps):
         need(q, deps)
         if q == "a":
-            return done("a", a.activation(out, win.indirect(lst), AF.Copy, scale=scale))
-        if scale == 1.0:
-            return done("v", v.tensor_copy(out, win.indirect(lst)))
-        return done("v", v.tensor_scalar(out, win.indirect(lst), scale, None, OP.mult))
+            return done("a", a.activation(out, win.indirect(lst), AF.Copy))
+        return done("v", v.tensor_copy(out, win.indirect(lst)))
 
     G = [[], [], [], []]
     E = [[], [], []]
     d = [None] * 4
+    e = [None] * 3
+    w = [None] * 3
     PT = [None] * 4
-    all_s = ("asn", 3 * 4 * ne)
+    PH = [None] * 3
+    all_s = ("asn", 3 * len(hp) * ne)
 
-    def GA(q, i, h0, h1):
-        G[i].append(gather(q, T["ga%d" % i][:, 512 * h0:512 * h1], T.fw[:, :], T.l1[:, 64 * i + 32 * h0:64 * i + 32 * h1], 1.0,
-                           t_fx, t_l1[i // 2]))
+    def GA(q, i, c0, c1):
+        if c0 < c1:
+            G[i].append(gather(q, T["ga%d" % i][:, 16 * c0:16 * c1], T.fw[:, :], T.l1[:, 64 * i + c0:64 * i + c1],
+                               tok["fx"], t_l1[i // 2]))
 
     def PE(i):
-        need("t", G[i] + [t_con1])
+        need("t", G[i] + [tok["w"]] + t_ev)
         for u in range(16):
             ins = t.matmul(T["ps%d" % i][:, 0:64], diag(u), T["ga%d" % i][:, u::16], u == 0, u == 15)
         PT[i] = done("t", ins)
 
-    def decide(i):
-        c, ps = slice(64 * i, 64 * i + 64), T["ps%d" % i][:, 0:64]
-        x = TT(T.acc[:, c], ps, T.b4[:, c], OP.is_gt, PT[i], t_b4)
-        x = TT(T.psv[:, c], T.ha[:, 64 * i + 64:64 * i + 128], ps, OP.subtract) if False else TT(T.psv[:, c], T.ha[:, 64 * i + 64:64 * i + 128], ps, OP.subtract)
-        x = TT(T.mm[:, c], T.acc[:, c], T.psv[:, c], OP.mult, x)
-        x = TT(T.xi[:, c], T.mm[:, c], ps, OP.add, x)
-        x = TS(T.ai[:, c], T.xi[:, c], 4095, OP.bitwise_and, None, None, x)
-        x = TT(T.cc[:, c], T.ai[:, c], q4, OP.add, x)
-        d[i] = CP(T.l2[:, c], T.cc[:, c], x) if i < 3 else x
+    def HI(q, i, c0, c1):
+        if c0 < c1:
+            E[i].append(gather(q, T["gb%d" % i][:, 16 * c0:16 * c1], T.sw[:, :], T.l2[:, 64 * i + c0:64 * i + c1],
+                               all_s, e[i], *t_ev))
 
-    def HI(q, i, h0, h1):
-        E[i].append(gather(q, T["gb%d" % i][:, 512 * h0:512 * h1], T.sw[:, :], T.l2[:, 64 * i + 32 * h0:64 * i + 32 * h1],
-                           float(16 ** (2 - i)), all_s, ld_sn[0], ld_sn[1], ld_sn[2], d[i]))
-
-    for i in range(3):
-        GA("a", i, 0, 1)
-        GA("v", i, 1, 2)
-        PE(i)
-    GA("a", 3, 0, 1)
-    decide(0)
-    HI("a", 0, 0, 2)
-    decide(1)
-    GA("v", 3, 1, 2)
-    PE(3)
-    HI("a", 1, 0, 2)
-    decide(2)
-    HI("v", 2, 0, 1)
-    decide(3)
-    HI("v", 2, 1, 2)
-    dc = T.psq[:, 64:256]
-    t_dc = TT(dc, T.cc[:, 64:256], T.cc[:, 0:192], OP.subtract, d[3])
-    CP(T.pp[:, 192:256], T.cc[:, 0:64])
-    for i in range(3):
-        need("t", E[i] + [t_con])
+    def PK(i):
+        need("t", E[i] + [tok["con"]])
         for u in range(16):
-            ins = t.matmul(T.psk[:, 0:64], T.cm[:, 127 * u:127 * u + 128], T["gb%d" % i][:, u::16], i + u == 0, i == 2 and u == 15)
-    t_psk = done("t", ins)
+            ins = t.matmul(T["ps%d" % i][:, 64:128], T.cm[:, 127 * u:127 * u + 128], T["gb%d" % i][:, u::16], u == 0, u == 15)
+        PH[i] = done("t", ins)
 
-    x = CP(T.vi[:, :], T.psk[:, 0:64], t_psk)
-    x = TS(T.vb[:, :], T.vi[:, :], rank, OP.logical_shift_right, 0x111, OP.bitwise_and, x)
-    for j, lim in enumerate((0x100, 0x110, 0x111)):
-        y = TS(T.mk[:, 64 * j:64 * j + 64], T.vb[:, :], float(lim), OP.is_ge, None, None, x)
-    x = TT(T.pp[:, 0:192], T.mk[:, :], dc, OP.mult, y, t_dc)
-    x = TT(T.p2[:, :], T.pp[:, 0:128], T.pp[:, 128:256], OP.add, x)
-    t_x = TT(T.xx[:, :], T.p2[:, 0:64], T.p2[:, 64:128], OP.add, x)
+    def decide(i):
+        c = slice(64 * i, 64 * i + 64)
+        m = {}
+
+        def f0():
+            tok[("x", i)] = TT(T.xi[:, c], T["ps%d" % i][:, 0:64], T.ce[:, c], OP.min, PT[i], t_ce)
+
+        def f1():
+            m[1] = TS(T.ah[:, c], T.xi[:, c], H - 1, OP.bitwise_and, None, None, tok[("x", i)])
+
+        def f2():
+            m[2] = TT(T.lh[:, c], T.ah[:, c], q2, OP.add, m[1], t_q2)
+
+        def f3():
+            e[i] = CP(T.l2[:, c], T.lh[:, c], m[2])
+
+        return [f0, f1, f2, f3] if i < 3 else [f0]
+
+    def name(i):
+        c = slice(64 * i, 64 * i + 64)
+        m = {}
+
+        def f0():
+            m[0] = TS(T.ai[:, c], T.xi[:, c], M - 1, OP.bitwise_and, None, None, tok[("x", i)])
+
+        def f1():
+            d[i] = TT(T.cc[:, c], T.ai[:, c], q4, OP.add, m[0])
+
+        def f2():
+            w[i] = TS(T.mh[:, c], T.ai[:, c], float(H), OP.is_lt, 0.0625, OP.max, m[0])
+
+        return [f0, f1, f2] if i < 3 else [f0, f1]
+
+    def run(*chains):
+        for k in range(max([len(c) for c in chains])):
+            for c in chains:
+                if k < len(c):
+                    c[k]()
+
+    for i in range(3):
+        GA("a", i, 0, 32)
+        GA("v", i, 32, 64)
+        PE(i)
+    GA("a", 3, 0, G3)
+    GA("v", 3, G3, 64)
+    PE(3)
+    run(decide(0), decide(1))
+    HI("a", 0, 0, HA[0])
+    run(decide(2), name(0), name(1))
+    HI("v", 0, HA[0], 64)
+    PK(0)
+    HI("v", 1, HA[1], 64)
+    HI("a", 1, 0, HA[1])
+    PK(1)
+    HI("a", 2, 0, HA[2])
+    run(decide(3), name(2))
+    HI("v", 2, HA[2], 64)
+    PK(2)
+    run(name(3))
+
+    bit = 16 << rank
+
+    def has(i):
+        c = slice(64 * i, 64 * i + 64)
+        x = TT(T.vi[:, c], T["ps%d" % i][:, 64:128], T.mh[:, c], OP.mult, PH[i], w[i])
+        return T.vb[:, c], TS(T.vb[:, c], T.vi[:, c], bit, OP.bitwise_and, None, None, x)
+
+    x = TT(T.psv[:, 0:192], T.cc[:, 64:256], T.cc[:, 0:192], OP.subtract, *d)
+    for i in range(3):
+        x = TS(T.psv[:, 192 + 64 * i:256 + 64 * i], T.psv[:, 64 * i:64 * i + 64], float(bit) ** (-1 - i), OP.mult, None, None, x)
+    t_dc = x
+    first, keep, rest = T.psq[:, 384:448], T.psq[:, 448:512], T.psk[:, 448:512]
+    b1, b2 = T.psk[:, 320:384], T.psk[:, 384:448]
+    s1, y = has(0)
+    x = TT(T.uu[:, 0:64], s1, T.psv[:, 192:256], OP.mult, y, t_dc)
+    t_b1 = TT(b1, s1, T.psv[:, 256:320], OP.mult)
+    t_b2 = TT(b2, s1, T.psv[:, 320:384], OP.mult)
+    x = TT(first, T.uu[:, 0:64], T.cc[:, 0:64], OP.add, x)
+    s2, y = has(1)
+    z = TT(T.uu[:, 64:128], s2, b1, OP.mult, y, t_b1)
+    t_r = TT(rest, s2, b2, OP.mult, t_b2)
+    t_k = TT(keep, T.uu[:, 64:128], first, OP.add, z, x)
+    s3, y = has(2)
+    y = TT(T.uu[:, 128:192], s3, rest, OP.mult, y, t_r)
+    t_x = TT(T.xx[:, :], T.uu[:, 128:192], keep, OP.add, y, t_k)
     t_l3 = CP(T.l3[:, :], T.xx[:, :], t_x)
     dma("s", T.chosen[:, :], T.xx[:, :], "st", t_x)
 
-    all_v = ("avc", 3 * 3 * ne)
-    ya = gather("a", T.yt[:, 512:1024], T.vw[:, :], T.l3[:, 32:64], 1.0, all_v, ld_v0, ld_v1, t_l3)
-    yv = gather("v", T.yt[:, 0:512], T.vw[:, :], T.l3[:, 0:32], 1.0, all_v, ld_v0, ld_v1, t_l3)
+    all_v = ("avc", 3 * len(vp) * ne)
+    ya = gather("a", T.yt[:, 512:1024], T.vw[:, :], T.l3[:, 32:64], all_v, t_l3, *ld_v)
+    yv = gather("v", T.yt[:, 0:512], T.vw[:, :], T.l3[:, 0:32], all_v, t_l3, *ld_v)
     dma("s", T.y[:, 0:512], T.yt[:, 0:512], "st", yv)
     t_st = dma("a", T.y[:, 512:1024], T.yt[:, 512:1024], "st", ya)
 
-    need("p", [("lr", lr)])
-    need("s", [t_st] + [(s, cnt[s]) for s in ("v", "a", "p", "t", "ldt", "lds", "ldr", "sn0", "sn1", "sn2", "vc0", "vc1", "fx")])
+    need("p", [("lr", lr[0])])
+    need("s", [t_st] + [(s, cnt[s]) for s in ("v", "a", "p", "t", "ldt", "lds", "ldr", "fx")])
+    need("s", ld_sn + ld_v)

@@ -5,17 +5,22 @@ M, K = 4096, 64
 H = M // 2
 MID = 1 << 24
 N1 = 1 << 23
-V_FILL = 5632
-P_FILL = 1024
+V_FILL = 2048
+P_FILL = [1024, 1024]
+V_LATE = 4096
 SRC = 1024
 HP = [0, 256, 1280, 2048]
 PP = [(0, 256, "psq", 0), (256, 768, "ps0", 1), (768, 1280, "ps1", 1), (1280, 1792, "ps2", 2), (1792, 2048, "ps3", 2)]
-A_FILLS = [4, 2, 1, 1, 0]
-VP = [(0, 896, 1), (896, 1792, 1), (1792, 4096, 0)]
-P_ORDER = ["h0", "t0", "t1", "t2", "fill", "w", "h1", "h2", "v0", "v1", "con", "v2"]
-S_ORDER = ["f0", "f1", "f2", "f3", "v0", "v1", "v2"]
-G3 = 48
-HA = [56, 40, 32]
+VP = [(0, 640, 1), (640, 1408, 1), (1408, 2176, 1), (2176, 4096, 0)]
+P_ORDER = "h0 t0 t1 t2 p0 h1 w h2 p1 v1 v2 con v3".split()
+S_ORDER = "f0 f1 f2 f3 v1 v2 v3".split()
+A_ORDER = "id4 fill fill fill e0 fill e1 xs e2 ys e3 e4 fill fill fill fill fill fill".split()
+V_ORDER = ("sdf shi X0 cf Y0 X1 k0 Y1 k1 X2 k2 X4 k3 X5 k4 X6 k5 XO Y2 Y4 Y5 Y6 X7 r0 r1 vf vf am cw X8 "
+           "g0 g1 g2 g3 g4 g5 g6 Y7 Y8 vf vf vf OFF ce cmz").split()
+GT = [32, 32, 32, 48]
+HA = [64, 40, 64]
+YS = [(0, 16, "v"), (32, 48, "a"), (16, 32, "v"), (48, 64, "a")]
+PB = ["ps2", "ps3", "psq"]
 W1 = 2048
 
 SCRATCH = {
@@ -31,27 +36,24 @@ SCRATCH = {
     "sdf": ("sbuf", [128, 1], "float32"),
     "cf": ("sbuf", [128, 1], "float32"),
     "rki": ("sbuf", [8, 8], "int32"),
-    "rkf": ("sbuf", [8, 8], "float32"),
+    "kc": ("sbuf", [8, 12], "float32"),
+    "rkf": ("sbuf", [8, 12], "float32"),
     "f8": ("sbuf", [8, 128], "float32"),
     "gs": ("sbuf", [8, 128], "float32"),
-    "a4": ("sbuf", [128, 4], "float32"),
-    "bt": ("sbuf", [128, 4], "float32"),
-    "j1": ("sbuf", [128, 4], "float32"),
-    "j4": ("sbuf", [128, 4], "float32"),
-    "dl": ("sbuf", [128, 8], "float32"),
     "am": ("sbuf", [128, 64], "int32"),
     "cw": ("sbuf", [128, 64], "float32"),
     "og": ("sbuf", [128, 448], "bfloat16"),
     "idt": ("sbuf", [128, 128], "bfloat16"),
+    "id4k": ("sbuf", [128, 128], "bfloat16"),
     "id16": ("sbuf", [128, 128], "bfloat16"),
     "cm": ("sbuf", [128, 2208], "bfloat16"),
     "n1": ("sbuf", [128, 320], "int32"),
     "hx": ("sbuf", [128, 320], "int32"),
     "hl": ("sbuf", [128, 320], "int32"),
     "hs": ("sbuf", [128, 320], "float32"),
-    "hm": ("sbuf", [128, 320], "int32"),
     "hs2": ("sbuf", [128, 320], "int32"),
     "hb": ("sbuf", [128, 320], "int32"),
+    "cb": ("sbuf", [128, 320], "float32"),
     "ht2": ("sbuf", [128, 320], "int32"),
     "ha": ("sbuf", [128, 320], "int32"),
     "ce": ("sbuf", [128, 256], "float32"),
@@ -61,7 +63,6 @@ SCRATCH = {
     "l3": ("sbuf", [128, 64], "uint16"),
     "xi": ("sbuf", [128, 256], "int32"),
     "ah": ("sbuf", [128, 192], "int32"),
-    "lh": ("sbuf", [128, 192], "float32"),
     "ai": ("sbuf", [128, 256], "int32"),
     "mh": ("sbuf", [128, 192], "float32"),
     "cc": ("sbuf", [128, 256], "float32"),
@@ -122,15 +123,14 @@ def helper_program(g, core, T, topo, owner):
     r = T.rank_of(owner)
     ne = len(topo.engines(owner, core))
     dsts = after(T, r)
+    hp, vp = hist(H * r), pieces(M * r)
+    order = [("v", 0)] + [("h", j) for j in range(len(hp))] + [("v", j) for j in range(1, len(vp)) if vp[j][2]]
     n = 0
-    for j, (x0, x1) in enumerate(hist(H * r)):
-        g.wait_ge(T.sem["hs%d" % j], ne)
-        n += spread(g, T, topo, core, dsts, T.sw[:, x0:x1], "asn", T.sw[:, x0:x1])
-    for j, (x0, x1, by) in enumerate(pieces(M * r)):
-        if not by:
-            continue
-        g.wait_ge(T.sem["hv%d" % j], ne)
-        n += spread(g, T, topo, core, dsts, T.vw[:, x0:x1], "avc", T.vw[:, x0:x1])
+    for c, j in order:
+        x0, x1 = (hp if c == "h" else vp)[j][:2]
+        win, arr, name = (T.sw, "hs%d" % j, "asn") if c == "h" else (T.vw, "hv%d" % j, "avc")
+        g.wait_ge(T.sem[arr], ne)
+        n += spread(g, T, topo, core, dsts, win[:, x0:x1], name, win[:, x0:x1])
     g.wait_ge(T.sem.lr, n)
 
 
@@ -146,6 +146,7 @@ def rank_program(g, core, T, topo):
     hc = helper_of(core, T, topo)
     ne = len(topo.engines(core, hc))
     b0 = M * rank
+    hp, vp = hist(H * rank), pieces(b0)
     engs = {"v": g.vector, "a": g.scalar, "p": g, "t": g.tensor, "s": g.sync}
     cnt = {}
     seen = {k: {} for k in engs}
@@ -186,6 +187,10 @@ def rank_program(g, core, T, topo):
         need("a", deps)
         return done("a", a.activation(out, x, AF.Copy, scale=scale))
 
+    def SQUARE(out, x, scale, bias, *deps):
+        need("a", deps)
+        return done("a", a.activation(out, x, AF.Square, bias=bias, scale=scale))
+
     def SEL(out, x, pattern, op, base, ch, *deps):
         need("p", deps)
         return done("p", g.affine_select(out, x, pattern, op, 0.0, base, ch))
@@ -200,15 +205,20 @@ def rank_program(g, core, T, topo):
     def send(dsts, win, x0, x1, sem):
         return spread(g, T, topo, core, dsts, win[:, x0:x1], sem, win[:, x0:x1])
 
+    ld_v = [None] * len(VP)
+
+    def s_vec(j):
+        x0, x1, by = vp[j]
+        ld_v[j] = dma("s", T.vw[:, x0:x1], T.vec[:, x0 - b0:x1 - b0], "vc%d" % j)
+
     def ld_seen(j):
-        for x in (0, H):
-            r = dma("s", T.sr[:, x + HP[j]:x + HP[j + 1]], T.seen[:, x + HP[j]:x + HP[j + 1]], "sn%d" % j)
-        return r
+        return dma("s", T.sr[:, 2 * HP[j]:2 * HP[j + 1]], T.seen[:, 2 * HP[j]:2 * HP[j + 1]], "sn%d" % j)
 
     ld_s = dma("a", T.sdi[:, :], T.sd[:, :], "lds")
+    s_vec(0)
     dma("s", T.ta[:, 256:512], T.ali[:, :], "ldt")
     ld_t = dma("a", T.ta[:, 0:256], T.thr[:, :], "ldt")
-    ld_r = dma("a", T.rki[:, :], T.rk[:, :], "ldr")
+    ld_r = dma("s", T.rki[:, :], T.rk[:, :], "ldr")
     ld_sn = [ld_seen(j) for j in range(len(HP) - 1)]
 
     regions = []
@@ -230,106 +240,165 @@ def rank_program(g, core, T, topo):
     t_src = FILL(T.fw[:, cs:cs + SRC], 1.0)
     regions.append((4 * M - SRC, 4 * M, t_src))
     t_f8 = FILL(T.f8[:, :], 1.0)
-    t_w0 = FILL(T.cm[:, W1:W1 + 144], 0.0)
     for x0, x1, c in blocks(0, V_FILL):
         regions.append((x0, x1, FILL(T.fw[:, c:c + x1 - x0], 1.0)))
+    t_w0 = FILL(T.cm[:, W1:W1 + 144], 0.0)
 
+    t_n1 = done("p", g.iota(T.n1[:, :], [[1597, 5], [5 * 1597, 64]], -N1, 0))
     t_id = SEL(T.idt[:, :], T.on[:, :], [[-1, 128]], OP.is_equal, 0, 1, t_on)
     t_id6 = SEL(T.id16[:, :], T.o16[:, :], [[-1, 128]], OP.is_equal, 0, 1, t_o16)
-    t_n1 = done("p", g.iota(T.n1[:, :], [[1597, 5], [5 * 1597, 64]], -N1, 0))
+    lr = [0]
+
+    def p_vec(j):
+        x0, x1, by = vp[j]
+        need("p", [ld_v[j]])
+        lr[0] += send([hc] if by else others, T.vw, x0, x1, "hv%d" % j if by else "avc")
+
+    p_vec(0)
+    CONST(T.kc[:, 0:4], [[M, 4]], 0)
+    CONST(T.kc[:, 4:8], [[-1, 4]], 0)
+    t_kc = CONST(T.kc[:, 8:11], [[1, 3]], 1)
     t_gs = SEL(T.gs[:, :], T.f8[:, :], [[1, 128]], OP.is_ge, 0, -16, t_f8)
     t_gs = SEL(T.gs[:, :], T.gs[:, :], [[-1, 128]], OP.is_ge, 15, 16, t_gs)
-    t_j4 = CONST(T.j4[:, :], [[M, 4]], 0)
-    t_j1 = CONST(T.j1[:, :], [[M // 4, 4]], 0)
 
-    def step(s, c0, c1):
-        c = slice(c0, c1)
-        k = lambda n: tok[(n, c0)]
-        if s == 0:
-            r = TS(T.hx[:, c], T.n1[:, c], T.sdf[:, 0:1], OP.add, None, None, t_n1, t_sdf)
-        elif s == 1:
-            r = TS(T.hl[:, c], T.hx[:, c], 4095, OP.bitwise_and, None, None, k(0))
-        elif s == 2:
-            r = TT(T.hs[:, c], T.hl[:, c], T.hl[:, c], OP.mult, k(1))
-        elif s == 3:
-            r = TS(T.hm[:, c], T.hl[:, c], 64.0, OP.mult, -float(1 << 22), OP.add, k(1))
-        elif s == 4:
-            r = TS(T.hs2[:, c], T.hs[:, c], T.cf[:, 0:1], OP.add, None, None, k(2), t_cf)
-        elif s == 5:
-            r = TS(T.hb[:, c], T.hs2[:, c], 6, OP.arith_shift_right, 4095, OP.bitwise_and, k(4))
-        elif s == 6:
-            r = TT(T.psk[:, c], T.hb[:, c], T.hb[:, c], OP.mult, k(5))
-        elif s == 7:
-            r = TT(T.ht2[:, c], T.psk[:, c], T.hm[:, c], OP.add, k(6), k(3))
-        else:
-            r = TS(T.ha[:, c], T.ht2[:, c], 6, OP.arith_shift_right, 4095, OP.bitwise_and, k(7))
-        tok[(s, c0)] = r
-        return r
-
-    def O(s):
-        return step(s, 0, 64)
-
-    def X(s):
-        return step(s, 64, 192)
-
-    def Y(s):
-        return step(s, 192, 320)
-
+    CH = {"X": (0, 192), "Y": (192, 320)}
+    sq = {"X": T.psk[:, 0:192], "Y": T.psq[:, 256:384]}
     pk = T.psv[:, 0:256]
     rp = T.psv[:, 256:512]
     t_p = [None] * 3
-    t_sdf = CP(T.sdf[:, :], T.sdi[:, :], ld_s)
-    t_shi = TS(T.shi[:, :], T.sdi[:, :], 12, OP.logical_shift_right, None, None)
-    x = TS(pk, T.ta[:, 0:256], float(2 * M), OP.mult, -float(MID), OP.add, ld_t)
-    t_cf = TS(T.cf[:, :], T.shi[:, :], 64.0, OP.mult, -float(1 << 22), OP.add, t_shi)
-    O(0)
-    x = TT(pk, pk, T.ta[:, 256:512], OP.add, x)
-    t_rkf = CP(T.rkf[:, :], T.rki[:, :], ld_r)
-    O(1)
-    t_p[0] = CP(T.ft[:, 0:256], pk, x)
-    X(0)
-    x = TT(rp, pk, T.ft[:, 0:256], OP.subtract, t_p[0])
-    Y(0)
-    t_p[1] = CP(T.ft[:, 256:512], rp, x)
-    O(2)
-    O(3)
-    t_p[2] = TT(T.ft[:, 512:768], rp, T.ft[:, 256:512], OP.subtract, t_p[1])
+    q4 = T.psr[:, 64:128]
+    t_l1 = [None, None]
+    vfills = [(c0, min(c0 + 1024, x1), c + c0 - x0) for x0, x1, c in blocks(4 * M - SRC - V_LATE, 4 * M - SRC)
+              for c0 in range(x0, x1, 1024)]
+
+    def hash_step(f, s):
+        c0, c1 = CH[f]
+        c = slice(c0, c1)
+        cc = slice(max(c0, 64), c1)
+        if s == "0":
+            r = TS(T.hx[:, c], T.n1[:, c], T.sdf[:, 0:1], OP.add, 64.0, OP.mult, t_n1, tok["sdf"])
+        elif s == "1":
+            r = TS(T.hl[:, c], T.hx[:, c], 64 * 4095, OP.bitwise_and, None, None, tok[f + "0"])
+        elif s == "2":
+            r = TT(T.hs[:, c], T.hl[:, c], T.hl[:, c], OP.mult, tok[f + "1"])
+        elif s == "4":
+            r = TS(T.hs2[:, c], T.hs[:, c], 1.0 / 4096, OP.mult, T.cf[:, 0:1], OP.add, tok[f + "2"], tok["cf"])
+        elif s == "5":
+            r = TS(T.hb[:, c], T.hs2[:, c], 6, OP.arith_shift_right, 4095, OP.bitwise_and, tok[f + "4"])
+        elif s == "6":
+            r = TS(T.cb[:, cc], T.hb[:, cc], float(2 * M), OP.mult, float(M - MID), OP.add, tok[f + "5"])
+        elif s == "O":
+            r = CP(T.cb[:, 0:64], T.hb[:, 0:64], tok[f + "5"])
+        elif s == "7":
+            r = TT(T.ht2[:, c], sq[f], T.hl[:, c], OP.add, tok[f + "s"])
+        elif s == "8":
+            r = TS(T.ha[:, cc], T.ht2[:, cc], 6, OP.arith_shift_right, 4095, OP.bitwise_and, tok[f + "7"])
+        tok[f + s] = r
+
+    def vop(n):
+        if n[0] in "XY":
+            hash_step(n[0], n[1])
+        elif n == "sdf":
+            tok[n] = CP(T.sdf[:, :], T.sdi[:, :], ld_s)
+        elif n == "shi":
+            tok[n] = TS(T.shi[:, :], T.sdi[:, :], 6, OP.logical_shift_right, 64 * 4095, OP.bitwise_and, ld_s)
+        elif n == "cf":
+            tok[n] = CP(T.cf[:, :], T.shi[:, :], tok["shi"])
+        elif n == "r0":
+            tok[n] = TT(T.rkf[:, 0:8], T.rki[:, :], T.kc[:, 0:8], OP.add, ld_r, t_kc)
+        elif n == "r1":
+            tok[n] = TT(T.rkf[:, 8:11], T.kc[:, 8:11], T.rki[:, 4:7], OP.subtract, ld_r, t_kc)
+        elif n == "k0":
+            tok[n] = TS(pk, T.ta[:, 0:256], float(2 * M), OP.mult, -float(MID), OP.add, ld_t)
+        elif n == "k1":
+            tok[n] = TT(pk, pk, T.ta[:, 256:512], OP.add, tok["k0"])
+        elif n == "k2":
+            t_p[0] = CP(T.ft[:, 0:256], pk, tok["k1"])
+        elif n == "k3":
+            tok[n] = TT(rp, pk, T.ft[:, 0:256], OP.subtract, t_p[0])
+        elif n == "k4":
+            t_p[1] = CP(T.ft[:, 256:512], rp, tok["k3"])
+        elif n == "k5":
+            t_p[2] = TT(T.ft[:, 512:768], rp, T.ft[:, 256:512], OP.subtract, t_p[1])
+        elif n == "am":
+            tok[n] = TS(T.am[:, :], T.ht2[:, 0:64], 4, OP.arith_shift_right, 12288, OP.bitwise_and, tok["X7"])
+        elif n == "cw":
+            tok[n] = TT(T.cw[:, :], T.am[:, :], T.cb[:, 0:64], OP.add, tok["am"], tok["XO"])
+        elif n[0] == "g":
+            j = int(n[1])
+            lim = T.psr[:, j:j + 1] if j < 4 else float(M * (j - 3))
+            tok["og"] = TS(T.og[:, 64 * j:64 * j + 64], T.cw[:, :], lim, OP.is_ge, T.psr[:, 4 + j:5 + j], OP.mult,
+                           tok["cw"], tok["psr"])
+        elif n == "ce":
+            tok[n] = TT(T.ce[:, :], T.cb[:, 64:320], T.ha[:, 64:320], OP.add, tok["X6"], tok["Y6"], tok["X8"], tok["Y8"])
+        elif n == "OFF":
+            x = [None] * 4
+            for i in range(4):
+                x[i] = TT(T.off[:, 64 * i:64 * i + 64], T.ha[:, 64 * i + 64:64 * i + 128], q4, OP.add, tok["q4"], tok["Y8"])
+                if i >= 2:
+                    h = i - 2
+                    t_l1[h] = CP(T.l1[:, 128 * h:128 * h + 128], T.off[:, 128 * h:128 * h + 128], x[2 * h + 1])
+        elif n == "cmz":
+            tok[n] = FILL(T.cm[:, 0:W1], 0.0)
+        elif n == "vf" and vfills:
+            x0, x1, c = vfills.pop(0)
+            regions.append((x0, x1, FILL(T.fw[:, c:c + x1 - x0], 1.0)))
 
     fills = []
-    c0 = V_FILL + P_FILL
-    while c0 < 4 * M - SRC:
-        c1 = min(4 * M - SRC, (c0 // 1024 + 1) * 1024)
+    c0 = V_FILL
+    while c0 < 4 * M - SRC - V_LATE - sum(P_FILL):
+        c1 = min(4 * M - SRC - V_LATE - sum(P_FILL), (c0 // 1024 + 1) * 1024)
         fills.append((c0, c1))
         c0 = c1
+    t_ev = [None] * len(PP)
 
-    def a_fill(n):
-        for c0, c1 in fills[:n]:
+    def aop(n):
+        if n == "fill":
+            c0, c1 = fills.pop(0)
             c = col(c0)
             regions.append((c0, c1, COPY(T.fw[:, c:c + c1 - c0], T.fw[:, cs:cs + c1 - c0], 1.0, t_src)))
-        del fills[:n]
+        elif n == "id4":
+            tok[n] = COPY(T.id4k[:, :], T.idt[:, :], float(M), t_id)
+        elif n[0] == "e":
+            j = int(n[1])
+            x0, x1, bank, grp = PP[j]
+            ps = T[bank][:, 0:x1 - x0]
+            need("t", [ld_sn[grp], t_id, t_id6])
+            t.matmul(ps, T.idt[:, :], T.sr[:, 2 * x0:2 * x1:2], True, False)
+            x = done("t", t.matmul(ps, T.id16[:, :], T.sr[:, 2 * x0 + 1:2 * x1:2], False, True))
+            t_ev[j] = COPY(T.sw[:, H * rank + x0:H * rank + x1], ps, 1.0, x)
+        elif n == "xs":
+            SQUARE(T.psk[:, 0:64], T.cb[:, 0:64], 1.0, 0.0, tok["XO"])
+            tok["Xs"] = SQUARE(T.psk[:, 64:192], T.cb[:, 64:192], 1.0 / (2 * M), 2047.5, tok["X6"])
+        elif n == "ys":
+            tok["Ys"] = SQUARE(sq["Y"], T.cb[:, 192:320], 1.0 / (2 * M), 2047.5, tok["Y6"])
 
-    t_ev = []
-    for j, (x0, x1, bank, grp) in enumerate(PP):
-        ps = T[bank][:, 0:x1 - x0]
-        need("t", [ld_sn[grp], t_id, t_id6])
-        t.matmul(ps, T.idt[:, :], T.sr[:, x0:x1], True, False)
-        x = done("t", t.matmul(ps, T.id16[:, :], T.sr[:, H + x0:H + x1], False, True))
-        if j == 0:
-            need("t", [t_rkf, t_gs])
-            t_psr = done("t", t.matmul(T.psr[:, 0:8], T.gs[:, :], T.rkf[:, :], True, True))
-        a_fill(A_FILLS[j])
-        t_ev.append(COPY(T.sw[:, H * rank + x0:H * rank + x1], ps, 1.0, x))
-    a_fill(len(fills))
-    for j in range(2):
-        t_zero = COPY(T.cm[:, 1024 * j:1024 * j + 1024], T.sr[:, 0:1024], 0.0, *ld_sn)
+    av = list(A_ORDER)
+    ready = {"xs": ["X6", "XO"], "ys": ["Y6"]}
 
-    hp = hist(H * rank)
-    vp = pieces(b0)
-    ld_v = [None] * len(vp)
+    def a_next():
+        while av and all([x in tok for x in ready.get(av[0], [])]):
+            n = av.pop(0)
+            if n != "fill" or fills:
+                aop(n)
 
-    def s_vec(j):
-        x0, x1, by = vp[j]
-        ld_v[j] = dma("s", T.vw[:, x0:x1], T.vec[:, x0 - b0:x1 - b0], "vc%d" % j)
+    a_next()
+    for n in V_ORDER:
+        vop(n)
+        if n == "r1":
+            need("t", [tok["r0"], tok["r1"], t_gs])
+            tok["psr"] = done("t", t.matmul(T.psr[:, 0:11], T.gs[:, :], T.rkf[:, 0:11], True, True))
+        if n == "g6":
+            need("t", [tok["og"], tok["id4"]])
+            for j in range(7):
+                ins = t.matmul(q4, T.id4k[:, :], T.og[:, 64 * j:64 * j + 64], j == 0, j == 6)
+            tok["q4"] = done("t", ins)
+        a_next()
+    while fills:
+        aop("fill")
+    while vfills:
+        vop("vf")
+    t_ce, t_zero = tok["ce"], tok["cmz"]
 
     def s_parts(k):
         q = (rank + k) % 4
@@ -341,7 +410,6 @@ def rank_program(g, core, T, topo):
             tok["fx"] = dma("s", T.fw[f::16, lo:hi], x, "fx", *deps)
 
     wm = T.cm[:, W1 + 15:W1 + 143:16]
-    lr = [0]
 
     def p_hist(j):
         need("p", [t_ev[i] for i in range(len(PP)) if PP[i][3] == j])
@@ -351,13 +419,9 @@ def rank_program(g, core, T, topo):
         need("p", [t_p[f]])
         lr[0] += spread(g, T, topo, core, others, T.ft[:, 256 * f:256 * f + 256], "aft%d" % rank, T.fl[3 * rank + f])
 
-    def p_vec(j):
-        x0, x1, by = vp[j]
-        need("p", [ld_v[j]])
-        lr[0] += send([hc] if by else others, T.vw, x0, x1, "hv%d" % j if by else "avc")
-
     def p_fill(j):
-        for y0, y1, c in blocks(V_FILL, V_FILL + P_FILL):
+        y = 4 * M - SRC - V_LATE - sum(P_FILL[j:])
+        for y0, y1, c in blocks(y, y + P_FILL[j]):
             regions.append((y0, y1, CONST(T.fw[:, c:c + y1 - y0], [[0, y1 - y0]], 1)))
 
     def p_w(j):
@@ -367,7 +431,7 @@ def rank_program(g, core, T, topo):
     def p_con(j):
         tok["con"] = SEL(T.cm[:, 0:2048:16], T.o16[:, :], [[-1, 16], [-16, 8]], OP.is_equal, 0, 1, t_zero)
 
-    calls = {"h": p_hist, "t": p_part, "v": p_vec, "fill": p_fill, "w": p_w, "con": p_con, "f": s_parts}
+    calls = {"h": p_hist, "t": p_part, "v": p_vec, "p": p_fill, "w": p_w, "con": p_con, "f": s_parts}
 
     def call(n):
         if n in calls:
@@ -394,59 +458,6 @@ def rank_program(g, core, T, topo):
     def diag(u):
         return T.cm[:, W1 + 15 - u:W1 + 143 - u]
 
-    def bt0():
-        tok["bt"] = TS(T.bt[:, :], T.psr[:, 0:4], 0.25, OP.mult, None, None, t_psr)
-
-    def a40():
-        tok["a4"] = TS(T.a4[:, :], T.psr[:, 4:8], float(M), OP.mult, None, None, t_psr)
-
-    def bt1():
-        tok["bt"] = TT(T.bt[:, :], T.bt[:, :], T.j1[:, :], OP.add, tok["bt"], t_j1)
-
-    def dl0():
-        TT(T.dl[:, 0:4], T.a4[:, :], T.j4[:, :], OP.subtract, tok["a4"], t_j4)
-        tok["dl"] = TT(T.dl[:, 4:7], T.j4[:, 1:4], T.a4[:, 0:3], OP.subtract)
-
-    def bq():
-        tok["bq"] = TS(T.psq[:, 0:64], T.hb[:, 0:64], 0.25, OP.mult, None, None, tok[(5, 0)], t_ev[0])
-
-    def am():
-        tok["am"] = TS(T.am[:, :], T.ht2[:, 0:64], 6, OP.arith_shift_right, 3072, OP.bitwise_and, tok[(7, 0)])
-
-    def cw():
-        tok["cw"] = TT(T.cw[:, :], T.am[:, :], T.psq[:, 0:64], OP.add, tok["am"], tok["bq"])
-
-    def og(j):
-        lim = T.bt[:, j:j + 1] if j < 4 else float(1024 * (j - 3))
-        tok["og"] = TS(T.og[:, 64 * j:64 * j + 64], T.cw[:, :], lim, OP.is_ge, T.dl[:, j:j + 1], OP.mult,
-                       tok["cw"], tok["bt"], tok["dl"])
-
-    own = [lambda: O(4), bt0, lambda: O(5), a40, lambda: O(6), bq, lambda: O(7), bt1, am, dl0, cw]
-    own += [lambda j=j: og(j) for j in range(7)]
-    cand = [lambda f=f, s=s: f(s) for s in range(1, 9) for f in (X, Y)]
-    while own or cand:
-        if own:
-            own.pop(0)()
-        if cand:
-            cand.pop(0)()
-    q4 = T.psr[:, 64:128]
-    q2 = T.psr[:, 128:192]
-    need("t", [tok["og"], t_id])
-    for j in range(7):
-        ins = t.matmul(q4, T.idt[:, :], T.og[:, 64 * j:64 * j + 64], j == 0, j == 6)
-    t_q4 = done("t", ins)
-    cb = T.psq[:, 128:384]
-    x = TS(cb, T.hb[:, 64:320], float(2 * M), OP.mult, float(M - MID), OP.add)
-    t_ce = TT(T.ce[:, :], cb, T.ha[:, 64:320], OP.add, x, tok[(8, 64)], tok[(8, 192)])
-    x = [None] * 4
-    t_l1 = [None, None]
-    for i in range(4):
-        x[i] = TT(T.off[:, 64 * i:64 * i + 64], T.ha[:, 64 * i + 64:64 * i + 128], q4, OP.add, t_q4)
-        if i >= 2:
-            h = i - 2
-            t_l1[h] = CP(T.l1[:, 128 * h:128 * h + 128], T.off[:, 128 * h:128 * h + 128], x[2 * h + 1])
-    t_q2 = TS(q2, q4, 0.5, OP.mult, None, None)
-
     def gather(q, out, win, lst, *deps):
         need(q, deps)
         if q == "a":
@@ -469,8 +480,9 @@ def rank_program(g, core, T, topo):
 
     def PE(i):
         need("t", G[i] + [tok["w"]] + t_ev)
+        out = T["ps%d" % (i // 2)][:, 64 * (i % 2):64 * (i % 2) + 64]
         for u in range(16):
-            ins = t.matmul(T["ps%d" % i][:, 0:64], diag(u), T["ga%d" % i][:, u::16], u == 0, u == 15)
+            ins = t.matmul(out, diag(u), T["ga%d" % i][:, u::16], u == 0, u == 15)
         PT[i] = done("t", ins)
 
     def HI(q, i, c0, c1):
@@ -481,81 +493,77 @@ def rank_program(g, core, T, topo):
     def PK(i):
         need("t", E[i] + [tok["con"]])
         for u in range(16):
-            ins = t.matmul(T["ps%d" % i][:, 64:128], T.cm[:, 127 * u:127 * u + 128], T["gb%d" % i][:, u::16], u == 0, u == 15)
+            ins = t.matmul(T[PB[i]][:, 256:320], T.cm[:, 127 * u:127 * u + 128], T["gb%d" % i][:, u::16], u == 0, u == 15)
         PH[i] = done("t", ins)
 
-    def decide(i):
-        c = slice(64 * i, 64 * i + 64)
+    def decide(j):
+        c = slice(128 * j, 128 * j + 128)
+        h = slice(128 * j, min(192, 128 * j + 128))
         m = {}
 
         def f0():
-            tok[("x", i)] = TT(T.xi[:, c], T["ps%d" % i][:, 0:64], T.ce[:, c], OP.min, PT[i], t_ce)
+            m[0] = TT(T.xi[:, c], T["ps%d" % j][:, 0:128], T.ce[:, c], OP.min, PT[2 * j + 1], t_ce)
 
         def f1():
-            m[1] = TS(T.ah[:, c], T.xi[:, c], H - 1, OP.bitwise_and, None, None, tok[("x", i)])
+            m[1] = TS(T.ai[:, c], T.xi[:, c], M - 1, OP.bitwise_and, None, None, m[0])
 
-        def f2():
-            m[2] = TT(T.lh[:, c], T.ah[:, c], q2, OP.add, m[1], t_q2)
+        def f2(i):
+            ci = slice(64 * i, 64 * i + 64)
+            d[i] = TT(T.cc[:, ci], T.ai[:, ci], q4, OP.add, m[1])
 
         def f3():
-            e[i] = CP(T.l2[:, c], T.lh[:, c], m[2])
+            x = TS(T.l2[:, h], T.cc[:, h], 0.5, OP.mult, -0.25, OP.add, d[2 * j], d[2 * j + (j == 0)])
+            for i in range(2 * j, min(3, 2 * j + 2)):
+                e[i] = x
 
-        return [f0, f1, f2, f3] if i < 3 else [f0]
+        def f4():
+            m[4] = TS(T.ah[:, h], T.xi[:, h], 1, OP.bitwise_and, None, None, m[0])
 
-    def name(i):
-        c = slice(64 * i, 64 * i + 64)
-        m = {}
+        def f5():
+            x = TS(T.mh[:, h], T.ah[:, h], -0.9375, OP.mult, 1.0, OP.add, m[4])
+            for i in range(2 * j, min(3, 2 * j + 2)):
+                w[i] = x
 
-        def f0():
-            m[0] = TS(T.ai[:, c], T.xi[:, c], M - 1, OP.bitwise_and, None, None, tok[("x", i)])
+        if j == 0:
+            return [f0, f1, lambda: f2(0), lambda: f2(1), f3], [f4, f5]
+        return [f0, f1, lambda: f2(2), f3], [lambda: f2(3), f4, f5]
 
-        def f1():
-            d[i] = TT(T.cc[:, c], T.ai[:, c], q4, OP.add, m[0])
+    def run(calls):
+        for f in calls:
+            f()
 
-        def f2():
-            w[i] = TS(T.mh[:, c], T.ai[:, c], float(H), OP.is_lt, 0.0625, OP.max, m[0])
-
-        return [f0, f1, f2] if i < 3 else [f0, f1]
-
-    def run(*chains):
-        for k in range(max([len(c) for c in chains])):
-            for c in chains:
-                if k < len(c):
-                    c[k]()
-
-    for i in range(3):
-        GA("a", i, 0, 32)
-        GA("v", i, 32, 64)
+    for i in range(4):
+        GA("a", i, 0, GT[i])
+        GA("v", i, GT[i], 64)
         PE(i)
-    GA("a", 3, 0, G3)
-    GA("v", 3, G3, 64)
-    PE(3)
-    run(decide(0), decide(1))
+    now, later = decide(0)
+    run(now)
     HI("a", 0, 0, HA[0])
-    run(decide(2), name(0), name(1))
+    HI("a", 1, 0, HA[1])
+    run(later)
     HI("v", 0, HA[0], 64)
     PK(0)
+    now, later = decide(1)
+    run(now)
     HI("v", 1, HA[1], 64)
-    HI("a", 1, 0, HA[1])
     PK(1)
     HI("a", 2, 0, HA[2])
-    run(decide(3), name(2))
+    run(later)
     HI("v", 2, HA[2], 64)
     PK(2)
-    run(name(3))
 
     bit = 16 << rank
 
     def has(i):
         c = slice(64 * i, 64 * i + 64)
-        x = TT(T.vi[:, c], T["ps%d" % i][:, 64:128], T.mh[:, c], OP.mult, PH[i], w[i])
+        x = TT(T.vi[:, c], T[PB[i]][:, 256:320], T.mh[:, c], OP.mult, PH[i], w[i])
         return T.vb[:, c], TS(T.vb[:, c], T.vi[:, c], bit, OP.bitwise_and, None, None, x)
 
     x = TT(T.psv[:, 0:192], T.cc[:, 64:256], T.cc[:, 0:192], OP.subtract, *d)
     for i in range(3):
         x = TS(T.psv[:, 192 + 64 * i:256 + 64 * i], T.psv[:, 64 * i:64 * i + 64], float(bit) ** (-1 - i), OP.mult, None, None, x)
     t_dc = x
-    first, keep, rest = T.psq[:, 384:448], T.psq[:, 448:512], T.psk[:, 448:512]
+    first, keep, rest = T.psr[:, 384:448], T.psr[:, 448:512], T.psk[:, 448:512]
     b1, b2 = T.psk[:, 320:384], T.psk[:, 384:448]
     s1, y = has(0)
     x = TT(T.uu[:, 0:64], s1, T.psv[:, 192:256], OP.mult, y, t_dc)
@@ -572,11 +580,12 @@ def rank_program(g, core, T, topo):
     t_l3 = CP(T.l3[:, :], T.xx[:, :], t_x)
     dma("s", T.chosen[:, :], T.xx[:, :], "st", t_x)
 
-    all_v = ("avc", 3 * len(vp) * ne)
-    ya = gather("a", T.yt[:, 512:1024], T.vw[:, :], T.l3[:, 32:64], all_v, t_l3, *ld_v)
-    yv = gather("v", T.yt[:, 0:512], T.vw[:, :], T.l3[:, 0:32], all_v, t_l3, *ld_v)
-    dma("s", T.y[:, 0:512], T.yt[:, 0:512], "st", yv)
-    t_st = dma("a", T.y[:, 512:1024], T.yt[:, 512:1024], "st", ya)
+    all_v = ("avc", 3 * len(VP) * ne)
+    yq = []
+    for c0, c1, q in YS:
+        yq.append((c0, c1, gather(q, T.yt[:, 16 * c0:16 * c1], T.vw[:, :], T.l3[:, c0:c1], all_v, t_l3, *ld_v)))
+    for c0, c1, x in yq:
+        t_st = dma("s", T.y[:, 16 * c0:16 * c1], T.yt[:, 16 * c0:16 * c1], "st", x)
 
     need("p", [("lr", lr[0])])
     need("s", [t_st] + [(s, cnt[s]) for s in ("v", "a", "p", "t", "ldt", "lds", "ldr", "fx")])

from concourse.bass import DstId, RemoteDMATransfer
from concourse.mybir import AluOpType as OP, ActivationFunctionType as AF

M, K = 4096, 64
H = M // 2
MID = 1 << 24
N1 = 1 << 23
V_FILL = 2048
P_FILL = [1024, 1024]
V_LATE = 4096
SRC = 1024
HP = [0, 256, 1280, 2048]
PP = [(0, 256, "psq", 0), (256, 768, "ps0", 1), (768, 1280, "ps1", 1), (1280, 1792, "ps2", 2), (1792, 2048, "ps3", 2)]
VP = [(0, 640, 1), (640, 1408, 1), (1408, 2176, 1), (2176, 4096, 0)]
P_ORDER = "h0 t0 t1 t2 p0 h1 w h2 p1 v1 v2 con v3".split()
S_ORDER = "f0 f1 f2 f3 v1 v2 v3".split()
A_ORDER = "id4 fill fill fill e0 fill e1 xs e2 ys e3 e4 fill fill fill fill fill fill".split()
V_ORDER = ("sdf shi X0 cf Y0 X1 k0 Y1 k1 X2 k2 X4 k3 X5 k4 X6 k5 XO Y2 Y4 Y5 Y6 X7 r0 r1 vf vf am cw X8 "
           "g0 g1 g2 g3 g4 g5 g6 Y7 Y8 vf vf vf OFF ce cmz").split()
GT = [32, 32, 32, 48]
HA = [64, 40, 64]
YS = [(0, 16, "v"), (32, 48, "a"), (16, 32, "v"), (48, 64, "a")]
PB = ["ps2", "ps3", "psq"]
W1 = 2048

SCRATCH = {
    "fw": ("sbuf", [128, 4 * M], "bfloat16"),
    "sr": ("sbuf", [128, M], "bfloat16"),
    "sw": ("sbuf", [128, 4 * H], "bfloat16"),
    "vw": ("sbuf", [128, 4 * M], "bfloat16"),
    "fl": ("dram", [12, 128, 256], "bfloat16"),
    "ta": ("sbuf", [128, 512], "int32"),
    "ft": ("sbuf", [128, 768], "bfloat16"),
    "sdi": ("sbuf", [128, 1], "int32"),
    "shi": ("sbuf", [128, 1], "int32"),
    "sdf": ("sbuf", [128, 1], "float32"),
    "cf": ("sbuf", [128, 1], "float32"),
    "rki": ("sbuf", [8, 8], "int32"),
    "kc": ("sbuf", [8, 12], "float32"),
    "rkf": ("sbuf", [8, 12], "float32"),
    "f8": ("sbuf", [8, 128], "float32"),
    "gs": ("sbuf", [8, 128], "float32"),
    "am": ("sbuf", [128, 64], "int32"),
    "cw": ("sbuf", [128, 64], "float32"),
    "og": ("sbuf", [128, 448], "bfloat16"),
    "idt": ("sbuf", [128, 128], "bfloat16"),
    "id4k": ("sbuf", [128, 128], "bfloat16"),
    "id16": ("sbuf", [128, 128], "bfloat16"),
    "cm": ("sbuf", [128, 2208], "bfloat16"),
    "n1": ("sbuf", [128, 320], "int32"),
    "hx": ("sbuf", [128, 320], "int32"),
    "hl": ("sbuf", [128, 320], "int32"),
    "hs": ("sbuf", [128, 320], "float32"),
    "hs2": ("sbuf", [128, 320], "int32"),
    "hb": ("sbuf", [128, 320], "int32"),
    "cb": ("sbuf", [128, 320], "float32"),
    "ht2": ("sbuf", [128, 320], "int32"),
    "ha": ("sbuf", [128, 320], "int32"),
    "ce": ("sbuf", [128, 256], "float32"),
    "off": ("sbuf", [128, 256], "float32"),
    "l1": ("sbuf", [128, 256], "uint16"),
    "l2": ("sbuf", [128, 192], "uint16"),
    "l3": ("sbuf", [128, 64], "uint16"),
    "xi": ("sbuf", [128, 256], "int32"),
    "ah": ("sbuf", [128, 192], "int32"),
    "ai": ("sbuf", [128, 256], "int32"),
    "mh": ("sbuf", [128, 192], "float32"),
    "cc": ("sbuf", [128, 256], "float32"),
    "vi": ("sbuf", [128, 192], "int32"),
    "vb": ("sbuf", [128, 192], "int32"),
    "uu": ("sbuf", [128, 192], "float32"),
    "xx": ("sbuf", [128, 64], "float32"),
    "yt": ("sbuf", [128, 1024], "bfloat16"),
    "on": ("sbuf", [128, 128], "bfloat16"),
    "o16": ("sbuf", [128, 128], "bfloat16"),
    "psr": ("psum", [128, 512], "float32"),
    "psv": ("psum", [128, 512], "float32"),
    "psq": ("psum", [128, 512], "float32"),
    "psk": ("psum", [128, 512], "float32"),
}
for _i in range(4):
    SCRATCH["ga%d" % _i] = ("sbuf", [128, 1024], "bfloat16")
    SCRATCH["ps%d" % _i] = ("psum", [128, 512], "float32")
for _i in range(3):
    SCRATCH["gb%d" % _i] = ("sbuf", [128, 1024], "bfloat16")

SEMAPHORES = ["v", "a", "p", "t", "ldt", "lds", "ldr", "fx", "st", "lr", "aft0", "aft1", "aft2", "aft3", "asn", "avc"]
SEMAPHORES += ["%s%d" % (s, j) for s in ("sn", "hs", "vc", "hv") for j in range(6)]


def helper_of(core, T, topo):
    free = [c for c in topo.cores_of(core) if T.rank_of(c) is None and topo.die(c) == topo.die(core)]
    mine = [c for c in T.cores if topo.chip(c) == topo.chip(core) and topo.die(c) == topo.die(core)]
    return free[mine.index(core)]


def spread(g, T, topo, core, dsts, src, name, dst_ap):
    ids = []
    for d in dsts:
        rid, pid, _s = topo.addr(d)
        ids.append(DstId(rid=rid, pnc=pid))
    mask = topo.mask(core, dsts[0])
    for d in dsts:
        mask &= topo.mask(core, d)
    g.remote_dma_fused([RemoteDMATransfer(dst_ids=ids, dma_engine_mask=mask, remote_sem=T.sem[name],
                                          srcs=[src], dsts=[dst_ap for d in dsts], alu_op=0)], local_sem=T.sem.lr)
    return len(topo.engines(core, dsts[0]))


def after(T, r):
    return [T.cores[(r + k) % len(T.cores)] for k in range(1, len(T.cores))]


def hist(b):
    return [(b + HP[j], b + HP[j + 1]) for j in range(len(HP) - 1)]


def pieces(b):
    return [(b + x0, b + x1, by) for x0, x1, by in VP]


def helper_program(g, core, T, topo, owner):
    r = T.rank_of(owner)
    ne = len(topo.engines(owner, core))
    dsts = after(T, r)
    hp, vp = hist(H * r), pieces(M * r)
    order = [("v", 0)] + [("h", j) for j in range(len(hp))] + [("v", j) for j in range(1, len(vp)) if vp[j][2]]
    n = 0
    for c, j in order:
        x0, x1 = (hp if c == "h" else vp)[j][:2]
        win, arr, name = (T.sw, "hs%d" % j, "asn") if c == "h" else (T.vw, "hv%d" % j, "avc")
        g.wait_ge(T.sem[arr], ne)
        n += spread(g, T, topo, core, dsts, win[:, x0:x1], name, win[:, x0:x1])
    g.wait_ge(T.sem.lr, n)


def rank_program(g, core, T, topo):
    rank = T.rank_of(core)
    if rank is None:
        for c in T.cores:
            if c in topo.cores_of(core) and helper_of(c, T, topo) == core:
                helper_program(g, core, T, topo, c)
        return

    others = after(T, rank)
    hc = helper_of(core, T, topo)
    ne = len(topo.engines(core, hc))
    b0 = M * rank
    hp, vp = hist(H * rank), pieces(b0)
    engs = {"v": g.vector, "a": g.scalar, "p": g, "t": g.tensor, "s": g.sync}
    cnt = {}
    seen = {k: {} for k in engs}
    tok = {}

    def need(q, toks):
        for name, val in toks:
            if seen[q].get(name, 0) < val:
                engs[q].wait_ge(T.sem[name], val)
                seen[q][name] = val

    def done(q, ins, n=1, sem=None):
        s = sem or q
        ins.then_inc(T.sem[s], n)
        cnt[s] = cnt.get(s, 0) + n
        return (s, cnt[s])

    v, a, t = g.vector, g.scalar, g.tensor

    def TT(out, x, y, op, *deps):
        need("v", deps)
        return done("v", v.tensor_tensor(out, x, y, op))

    def TS(out, x, s1, op0, s2, op1, *deps):
        need("v", deps)
        if op1 is None:
            return done("v", v.tensor_scalar(out, x, s1, None, op0))
        return done("v", v.tensor_scalar(out, x, s1, s2, op0, op1))

    def CP(out, x, *deps):
        need("v", deps)
        return done("v", v.tensor_copy(out, x))

    def FILL(ap, c):
        return done("v", v.memset(ap, c))

    def COPY(out, x, scale, *deps):
        need("a", deps)
        return done("a", a.activation(out, x, AF.Copy, scale=scale))

    def SQUARE(out, x, scale, bias, *deps):
        need("a", deps)
        return done("a", a.activation(out, x, AF.Square, bias=bias, scale=scale))

    def SEL(out, x, pattern, op, base, ch, *deps):
        need("p", deps)
        return done("p", g.affine_select(out, x, pattern, op, 0.0, base, ch))

    def CONST(out, pattern, c):
        return done("p", g.iota(out, pattern, c, 0, allow_small_or_imprecise_dtypes=True))

    def dma(q, out, x, sem, *deps):
        need(q, deps)
        return done(q, engs[q].dma_start(out, x), 16, sem)

    def send(dsts, win, x0, x1, sem):
        return spread(g, T, topo, core, dsts, win[:, x0:x1], sem, win[:, x0:x1])

    ld_v = [None] * len(VP)

    def s_vec(j):
        x0, x1, by = vp[j]
        ld_v[j] = dma("s", T.vw[:, x0:x1], T.vec[:, x0 - b0:x1 - b0], "vc%d" % j)

    def ld_seen(j):
        return dma("s", T.sr[:, 2 * HP[j]:2 * HP[j + 1]], T.seen[:, 2 * HP[j]:2 * HP[j + 1]], "sn%d" % j)

    ld_s = dma("a", T.sdi[:, :], T.sd[:, :], "lds")
    s_vec(0)
    dma("s", T.ta[:, 256:512], T.ali[:, :], "ldt")
    ld_t = dma("a", T.ta[:, 0:256], T.thr[:, :], "ldt")
    ld_r = dma("s", T.rki[:, :], T.rk[:, :], "ldr")
    ld_sn = [ld_seen(j) for j in range(len(HP) - 1)]

    regions = []

    def col(x):
        return (b0 + x) % (4 * M)

    def blocks(x0, x1):
        out = []
        while x0 < x1:
            e = min(x1, (x0 // M + 1) * M)
            out.append((x0, e, col(x0)))
            x0 = e
        return out

    cs = col(4 * M - SRC)
    t_on = FILL(T.on[:, :], 1.0)
    t_o16 = FILL(T.o16[:, :], 16.0)
    t_src = FILL(T.fw[:, cs:cs + SRC], 1.0)
    regions.append((4 * M - SRC, 4 * M, t_src))
    t_f8 = FILL(T.f8[:, :], 1.0)
    for x0, x1, c in blocks(0, V_FILL):
        regions.append((x0, x1, FILL(T.fw[:, c:c + x1 - x0], 1.0)))
    t_w0 = FILL(T.cm[:, W1:W1 + 144], 0.0)

    t_n1 = done("p", g.iota(T.n1[:, :], [[1597, 5], [5 * 1597, 64]], -N1, 0))
    t_id = SEL(T.idt[:, :], T.on[:, :], [[-1, 128]], OP.is_equal, 0, 1, t_on)
    t_id6 = SEL(T.id16[:, :], T.o16[:, :], [[-1, 128]], OP.is_equal, 0, 1, t_o16)
    lr = [0]

    def p_vec(j):
        x0, x1, by = vp[j]
        need("p", [ld_v[j]])
        lr[0] += send([hc] if by else others, T.vw, x0, x1, "hv%d" % j if by else "avc")

    p_vec(0)
    CONST(T.kc[:, 0:4], [[M, 4]], 0)
    CONST(T.kc[:, 4:8], [[-1, 4]], 0)
    t_kc = CONST(T.kc[:, 8:11], [[1, 3]], 1)
    t_gs = SEL(T.gs[:, :], T.f8[:, :], [[1, 128]], OP.is_ge, 0, -16, t_f8)
    t_gs = SEL(T.gs[:, :], T.gs[:, :], [[-1, 128]], OP.is_ge, 15, 16, t_gs)

    CH = {"X": (0, 192), "Y": (192, 320)}
    sq = {"X": T.psk[:, 0:192], "Y": T.psq[:, 256:384]}
    pk = T.psv[:, 0:256]
    rp = T.psv[:, 256:512]
    t_p = [None] * 3
    q4 = T.psr[:, 64:128]
    t_l1 = [None, None]
    vfills = [(c0, min(c0 + 1024, x1), c + c0 - x0) for x0, x1, c in blocks(4 * M - SRC - V_LATE, 4 * M - SRC)
              for c0 in range(x0, x1, 1024)]

    def hash_step(f, s):
        c0, c1 = CH[f]
        c = slice(c0, c1)
        cc = slice(max(c0, 64), c1)
        if s == "0":
            r = TS(T.hx[:, c], T.n1[:, c], T.sdf[:, 0:1], OP.add, 64.0, OP.mult, t_n1, tok["sdf"])
        elif s == "1":
            r = TS(T.hl[:, c], T.hx[:, c], 64 * 4095, OP.bitwise_and, None, None, tok[f + "0"])
        elif s == "2":
            r = TT(T.hs[:, c], T.hl[:, c], T.hl[:, c], OP.mult, tok[f + "1"])
        elif s == "4":
            r = TS(T.hs2[:, c], T.hs[:, c], 1.0 / 4096, OP.mult, T.cf[:, 0:1], OP.add, tok[f + "2"], tok["cf"])
        elif s == "5":
            r = TS(T.hb[:, c], T.hs2[:, c], 6, OP.arith_shift_right, 4095, OP.bitwise_and, tok[f + "4"])
        elif s == "6":
            r = TS(T.cb[:, cc], T.hb[:, cc], float(2 * M), OP.mult, float(M - MID), OP.add, tok[f + "5"])
        elif s == "O":
            r = CP(T.cb[:, 0:64], T.hb[:, 0:64], tok[f + "5"])
        elif s == "7":
            r = TT(T.ht2[:, c], sq[f], T.hl[:, c], OP.add, tok[f + "s"])
        elif s == "8":
            r = TS(T.ha[:, cc], T.ht2[:, cc], 6, OP.arith_shift_right, 4095, OP.bitwise_and, tok[f + "7"])
        tok[f + s] = r

    def vop(n):
        if n[0] in "XY":
            hash_step(n[0], n[1])
        elif n == "sdf":
            tok[n] = CP(T.sdf[:, :], T.sdi[:, :], ld_s)
        elif n == "shi":
            tok[n] = TS(T.shi[:, :], T.sdi[:, :], 6, OP.logical_shift_right, 64 * 4095, OP.bitwise_and, ld_s)
        elif n == "cf":
            tok[n] = CP(T.cf[:, :], T.shi[:, :], tok["shi"])
        elif n == "r0":
            tok[n] = TT(T.rkf[:, 0:8], T.rki[:, :], T.kc[:, 0:8], OP.add, ld_r, t_kc)
        elif n == "r1":
            tok[n] = TT(T.rkf[:, 8:11], T.kc[:, 8:11], T.rki[:, 4:7], OP.subtract, ld_r, t_kc)
        elif n == "k0":
            tok[n] = TS(pk, T.ta[:, 0:256], float(2 * M), OP.mult, -float(MID), OP.add, ld_t)
        elif n == "k1":
            tok[n] = TT(pk, pk, T.ta[:, 256:512], OP.add, tok["k0"])
        elif n == "k2":
            t_p[0] = CP(T.ft[:, 0:256], pk, tok["k1"])
        elif n == "k3":
            tok[n] = TT(rp, pk, T.ft[:, 0:256], OP.subtract, t_p[0])
        elif n == "k4":
            t_p[1] = CP(T.ft[:, 256:512], rp, tok["k3"])
        elif n == "k5":
            t_p[2] = TT(T.ft[:, 512:768], rp, T.ft[:, 256:512], OP.subtract, t_p[1])
        elif n == "am":
            tok[n] = TS(T.am[:, :], T.ht2[:, 0:64], 4, OP.arith_shift_right, 12288, OP.bitwise_and, tok["X7"])
        elif n == "cw":
            tok[n] = TT(T.cw[:, :], T.am[:, :], T.cb[:, 0:64], OP.add, tok["am"], tok["XO"])
        elif n[0] == "g":
            j = int(n[1])
            lim = T.psr[:, j:j + 1] if j < 4 else float(M * (j - 3))
            tok["og"] = TS(T.og[:, 64 * j:64 * j + 64], T.cw[:, :], lim, OP.is_ge, T.psr[:, 4 + j:5 + j], OP.mult,
                           tok["cw"], tok["psr"])
        elif n == "ce":
            tok[n] = TT(T.ce[:, :], T.cb[:, 64:320], T.ha[:, 64:320], OP.add, tok["X6"], tok["Y6"], tok["X8"], tok["Y8"])
        elif n == "OFF":
            x = [None] * 4
            for i in range(4):
                x[i] = TT(T.off[:, 64 * i:64 * i + 64], T.ha[:, 64 * i + 64:64 * i + 128], q4, OP.add, tok["q4"], tok["Y8"])
                if i >= 2:
                    h = i - 2
                    t_l1[h] = CP(T.l1[:, 128 * h:128 * h + 128], T.off[:, 128 * h:128 * h + 128], x[2 * h + 1])
        elif n == "cmz":
            tok[n] = FILL(T.cm[:, 0:W1], 0.0)
        elif n == "vf" and vfills:
            x0, x1, c = vfills.pop(0)
            regions.append((x0, x1, FILL(T.fw[:, c:c + x1 - x0], 1.0)))

    fills = []
    c0 = V_FILL
    while c0 < 4 * M - SRC - V_LATE - sum(P_FILL):
        c1 = min(4 * M - SRC - V_LATE - sum(P_FILL), (c0 // 1024 + 1) * 1024)
        fills.append((c0, c1))
        c0 = c1
    t_ev = [None] * len(PP)

    def aop(n):
        if n == "fill":
            c0, c1 = fills.pop(0)
            c = col(c0)
            regions.append((c0, c1, COPY(T.fw[:, c:c + c1 - c0], T.fw[:, cs:cs + c1 - c0], 1.0, t_src)))
        elif n == "id4":
            tok[n] = COPY(T.id4k[:, :], T.idt[:, :], float(M), t_id)
        elif n[0] == "e":
            j = int(n[1])
            x0, x1, bank, grp = PP[j]
            ps = T[bank][:, 0:x1 - x0]
            need("t", [ld_sn[grp], t_id, t_id6])
            t.matmul(ps, T.idt[:, :], T.sr[:, 2 * x0:2 * x1:2], True, False)
            x = done("t", t.matmul(ps, T.id16[:, :], T.sr[:, 2 * x0 + 1:2 * x1:2], False, True))
            t_ev[j] = COPY(T.sw[:, H * rank + x0:H * rank + x1], ps, 1.0, x)
        elif n == "xs":
            SQUARE(T.psk[:, 0:64], T.cb[:, 0:64], 1.0, 0.0, tok["XO"])
            tok["Xs"] = SQUARE(T.psk[:, 64:192], T.cb[:, 64:192], 1.0 / (2 * M), 2047.5, tok["X6"])
        elif n == "ys":
            tok["Ys"] = SQUARE(sq["Y"], T.cb[:, 192:320], 1.0 / (2 * M), 2047.5, tok["Y6"])

    av = list(A_ORDER)
    ready = {"xs": ["X6", "XO"], "ys": ["Y6"]}

    def a_next():
        while av and all([x in tok for x in ready.get(av[0], [])]):
            n = av.pop(0)
            if n != "fill" or fills:
                aop(n)

    a_next()
    for n in V_ORDER:
        vop(n)
        if n == "r1":
            need("t", [tok["r0"], tok["r1"], t_gs])
            tok["psr"] = done("t", t.matmul(T.psr[:, 0:11], T.gs[:, :], T.rkf[:, 0:11], True, True))
        if n == "g6":
            need("t", [tok["og"], tok["id4"]])
            for j in range(7):
                ins = t.matmul(q4, T.id4k[:, :], T.og[:, 64 * j:64 * j + 64], j == 0, j == 6)
            tok["q4"] = done("t", ins)
        a_next()
    while fills:
        aop("fill")
    while vfills:
        vop("vf")
    t_ce, t_zero = tok["ce"], tok["cmz"]

    def s_parts(k):
        q = (rank + k) % 4
        lo, hi = M * q, M * q + M
        deps = [tk for (x0, x1, tk) in regions if x0 < M * k + M and M * k < x1]
        deps += [t_p[2]] if k == 0 else [("aft%d" % q, 3 * len(topo.engines(T.cores[q], core)))]
        for f in range(3):
            x = T.ft[:, 256 * f:256 * f + 256] if k == 0 else T.fl[3 * q + f]
            tok["fx"] = dma("s", T.fw[f::16, lo:hi], x, "fx", *deps)

    wm = T.cm[:, W1 + 15:W1 + 143:16]

    def p_hist(j):
        need("p", [t_ev[i] for i in range(len(PP)) if PP[i][3] == j])
        lr[0] += send([hc], T.sw, hp[j][0], hp[j][1], "hs%d" % j)

    def p_part(f):
        need("p", [t_p[f]])
        lr[0] += spread(g, T, topo, core, others, T.ft[:, 256 * f:256 * f + 256], "aft%d" % rank, T.fl[3 * rank + f])

    def p_fill(j):
        y = 4 * M - SRC - V_LATE - sum(P_FILL[j:])
        for y0, y1, c in blocks(y, y + P_FILL[j]):
            regions.append((y0, y1, CONST(T.fw[:, c:c + y1 - y0], [[0, y1 - y0]], 1)))

    def p_w(j):
        x = SEL(wm, T.on[:, 0:8], [[-16, 8]], OP.is_ge, 0, 1, t_w0)
        tok["w"] = SEL(wm, wm, [[16, 8]], OP.is_ge, 2, -1, x)

    def p_con(j):
        tok["con"] = SEL(T.cm[:, 0:2048:16], T.o16[:, :], [[-1, 16], [-16, 8]], OP.is_equal, 0, 1, t_zero)

    calls = {"h": p_hist, "t": p_part, "v": p_vec, "p": p_fill, "w": p_w, "con": p_con, "f": s_parts}

    def call(n):
        if n in calls:
            calls[n](0)
        else:
            calls[n[0]](int(n[1:]))

    todo = list(S_ORDER)

    def s_next():
        n = todo.pop(0)
        if n[0] == "v":
            s_vec(int(n[1:]))
        else:
            call(n)

    for n in P_ORDER:
        while n[0] == "v" and ld_v[int(n[1:])] is None:
            s_next()
        call(n)
    while todo:
        s_next()

    def diag(u):
        return T.cm[:, W1 + 15 - u:W1 + 143 - u]

    def gather(q, out, win, lst, *deps):
        need(q, deps)
        if q == "a":
            return done("a", a.activation(out, win.indirect(lst), AF.Copy))
        return done("v", v.tensor_copy(out, win.indirect(lst)))

    G = [[], [], [], []]
    E = [[], [], []]
    d = [None] * 4
    e = [None] * 3
    w = [None] * 3
    PT = [None] * 4
    PH = [None] * 3
    all_s = ("asn", 3 * len(hp) * ne)

    def GA(q, i, c0, c1):
        if c0 < c1:
            G[i].append(gather(q, T["ga%d" % i][:, 16 * c0:16 * c1], T.fw[:, :], T.l1[:, 64 * i + c0:64 * i + c1],
                               tok["fx"], t_l1[i // 2]))

    def PE(i):
        need("t", G[i] + [tok["w"]] + t_ev)
        out = T["ps%d" % (i // 2)][:, 64 * (i % 2):64 * (i % 2) + 64]
        for u in range(16):
            ins = t.matmul(out, diag(u), T["ga%d" % i][:, u::16], u == 0, u == 15)
        PT[i] = done("t", ins)

    def HI(q, i, c0, c1):
        if c0 < c1:
            E[i].append(gather(q, T["gb%d" % i][:, 16 * c0:16 * c1], T.sw[:, :], T.l2[:, 64 * i + c0:64 * i + c1],
                               all_s, e[i], *t_ev))

    def PK(i):
        need("t", E[i] + [tok["con"]])
        for u in range(16):
            ins = t.matmul(T[PB[i]][:, 256:320], T.cm[:, 127 * u:127 * u + 128], T["gb%d" % i][:, u::16], u == 0, u == 15)
        PH[i] = done("t", ins)

    def decide(j):
        c = slice(128 * j, 128 * j + 128)
        h = slice(128 * j, min(192, 128 * j + 128))
        m = {}

        def f0():
            m[0] = TT(T.xi[:, c], T["ps%d" % j][:, 0:128], T.ce[:, c], OP.min, PT[2 * j + 1], t_ce)

        def f1():
            m[1] = TS(T.ai[:, c], T.xi[:, c], M - 1, OP.bitwise_and, None, None, m[0])

        def f2(i):
            ci = slice(64 * i, 64 * i + 64)
            d[i] = TT(T.cc[:, ci], T.ai[:, ci], q4, OP.add, m[1])

        def f3():
            x = TS(T.l2[:, h], T.cc[:, h], 0.5, OP.mult, -0.25, OP.add, d[2 * j], d[2 * j + (j == 0)])
            for i in range(2 * j, min(3, 2 * j + 2)):
                e[i] = x

        def f4():
            m[4] = TS(T.ah[:, h], T.xi[:, h], 1, OP.bitwise_and, None, None, m[0])

        def f5():
            x = TS(T.mh[:, h], T.ah[:, h], -0.9375, OP.mult, 1.0, OP.add, m[4])
            for i in range(2 * j, min(3, 2 * j + 2)):
                w[i] = x

        if j == 0:
            return [f0, f1, lambda: f2(0), lambda: f2(1), f3], [f4, f5]
        return [f0, f1, lambda: f2(2), f3], [lambda: f2(3), f4, f5]

    def run(calls):
        for f in calls:
            f()

    for i in range(4):
        GA("a", i, 0, GT[i])
        GA("v", i, GT[i], 64)
        PE(i)
    now, later = decide(0)
    run(now)
    HI("a", 0, 0, HA[0])
    HI("a", 1, 0, HA[1])
    run(later)
    HI("v", 0, HA[0], 64)
    PK(0)
    now, later = decide(1)
    run(now)
    HI("v", 1, HA[1], 64)
    PK(1)
    HI("a", 2, 0, HA[2])
    run(later)
    HI("v", 2, HA[2], 64)
    PK(2)

    bit = 16 << rank

    def has(i):
        c = slice(64 * i, 64 * i + 64)
        x = TT(T.vi[:, c], T[PB[i]][:, 256:320], T.mh[:, c], OP.mult, PH[i], w[i])
        return T.vb[:, c], TS(T.vb[:, c], T.vi[:, c], bit, OP.bitwise_and, None, None, x)

    x = TT(T.psv[:, 0:192], T.cc[:, 64:256], T.cc[:, 0:192], OP.subtract, *d)
    for i in range(3):
        x = TS(T.psv[:, 192 + 64 * i:256 + 64 * i], T.psv[:, 64 * i:64 * i + 64], float(bit) ** (-1 - i), OP.mult, None, None, x)
    t_dc = x
    first, keep, rest = T.psr[:, 384:448], T.psr[:, 448:512], T.psk[:, 448:512]
    b1, b2 = T.psk[:, 320:384], T.psk[:, 384:448]
    s1, y = has(0)
    x = TT(T.uu[:, 0:64], s1, T.psv[:, 192:256], OP.mult, y, t_dc)
    t_b1 = TT(b1, s1, T.psv[:, 256:320], OP.mult)
    t_b2 = TT(b2, s1, T.psv[:, 320:384], OP.mult)
    x = TT(first, T.uu[:, 0:64], T.cc[:, 0:64], OP.add, x)
    s2, y = has(1)
    z = TT(T.uu[:, 64:128], s2, b1, OP.mult, y, t_b1)
    t_r = TT(rest, s2, b2, OP.mult, t_b2)
    t_k = TT(keep, T.uu[:, 64:128], first, OP.add, z, x)
    s3, y = has(2)
    y = TT(T.uu[:, 128:192], s3, rest, OP.mult, y, t_r)
    t_x = TT(T.xx[:, :], T.uu[:, 128:192], keep, OP.add, y, t_k)
    t_l3 = CP(T.l3[:, :], T.xx[:, :], t_x)
    dma("s", T.chosen[:, :], T.xx[:, :], "st", t_x)

    all_v = ("avc", 3 * len(VP) * ne)
    yq = []
    for c0, c1, q in YS:
        yq.append((c0, c1, gather(q, T.yt[:, 16 * c0:16 * c1], T.vw[:, :], T.l3[:, c0:c1], all_v, t_l3, *ld_v)))
    for c0, c1, x in yq:
        t_st = dma("s", T.y[:, 16 * c0:16 * c1], T.yt[:, 16 * c0:16 * c1], "st", x)

    need("p", [("lr", lr[0])])
    need("s", [t_st] + [(s, cnt[s]) for s in ("v", "a", "p", "t", "ldt", "lds", "ldr", "fx")])
    need("s", ld_sn + ld_v)
